import numpy as np, ml_dtypes
CORES = [9,25,41,57]
N = 4
import mx_ref
BF = ml_dtypes.bfloat16
def gcols(t, e):
    v = np.concatenate([t.reshape(8, 16, -1, 4), np.zeros((8, 16, 1, 4), BF)], axis=2)
    return np.ascontiguousarray(np.stack([v[g][:, e[g]] for g in range(8)])).reshape(128, -1)
def tile(rs):
    return np.stack(rs, axis=2).reshape(128, -1).astype(BF)
def pick(q, e):
    c = np.concatenate([q[0].reshape(128, -1, 4), np.zeros((128, 1, 4), np.uint8)], axis=1); s = np.concatenate([q[1], np.ones((16, 1), np.uint8)], axis=1)
    return (np.ascontiguousarray(c[:, e].reshape(128, -1)), np.ascontiguousarray(s[:, e]))
def join(*qs):
    return (np.concatenate([q[0] for q in qs], axis=1), np.concatenate([q[1] for q in qs], axis=1))
def put(q, e, v):
    c, s = q[0].reshape(128, -1, 4).copy(), q[1].copy(); c[:, e] = v[0].reshape(128, -1, 4); s[:, e] = v[1]
    return (c.reshape(128, -1), s)
def pk(c, s):
    return (np.ascontiguousarray(c), mx_ref.live(s))
def emit(q):
    return q[0], q[1]
def packed(v, rng):
    q = [mx_ref.quantize(np.ascontiguousarray(v[r])) for r in range(N)]
    return np.stack([a for a, b in q]), np.stack([mx_ref.plane(b, rng) for a, b in q])
def values_of_codes():
    e, c = np.zeros((128, 128, 4), np.float32), np.zeros((128, 2, 4), np.uint8)
    e[np.arange(128), np.arange(128), 0] = 1
    c[:127, :, 0] = np.arange(256).reshape(2, 128).T[:127]
    return mx_ref.matmul(mx_ref.quantize(e.reshape(128, 512).astype(BF)), (c.reshape(128, 8), np.full((16, 2), 127, np.uint8))).T.reshape(-1).astype(np.float64)
CODE_VALUE, SCALE_VALUE = values_of_codes(), 2.0 ** (np.arange(256) - 127.0)
def decode(q):
    return (CODE_VALUE[q[0]].reshape(16, 8, -1, 4) * SCALE_VALUE[q[1]][:, None, :, None] + 0.0).reshape(128, -1).astype(np.float32)
def f(rng, *shape):
    return mx_ref.flush((rng.standard_normal(shape, dtype=np.float32) * np.exp2(rng.integers(-2, 3, shape[:-1] + (1,)))).astype(BF))
def wide(rng, *shape, cols=0):
    v = rng.standard_normal(shape, dtype=np.float32) * np.exp2(rng.integers(-12, 13, shape)).astype(np.float32)
    if cols: v *= np.repeat(np.exp2(rng.integers(-cols, cols + 1, shape[:-2] + (1, shape[-1] // 4))) * (rng.random(shape[:-2] + (1, shape[-1] // 4)) > 0.0625), 4, axis=-1).astype(np.float32)
    return mx_ref.flush(v.astype(BF))
C, L, R = 320, 96, 3
def big(v):
    v = v.astype(np.float32)
    v[np.abs(v) < np.float32(2.0 ** -16)] = 0
    return v.astype(BF)
def numbers_of(rng):
    return {"x": big(f(rng, N, 128, 4 * C)), "u": np.array(f(rng, N, 128, 512)), "v": np.array(f(rng, N, 128, 512))}
def layers(rng):
    return big(f(rng, N, 128, 2048)).reshape(N, 8, 16, 4, 8, 16, 4)
def weights(rng, w):
    c, p = packed(np.ascontiguousarray(w).reshape(N, 128, 2048), rng)
    return {"wc": c, "ws": p}
def setup_inputs(rng):
    return {**numbers_of(rng), **weights(rng, layers(rng))}
def setup_inputs_ties(rng):
    d = numbers_of(rng)
    x = d["x"].reshape(N, 8, 16, C, 4)
    x[:, :, 0] = 0
    x[:, :, 0, :, 0] = np.floor(rng.integers(2, 7, (N, 8, 1)) * rng.random((N, 8, C))).astype(np.float32).astype(BF)
    u = d["u"].reshape(N, 128, 128, 4)
    u[:, :, ::16] = 0
    o = rng.permutation(N)
    for r in range(N):
        for h in range(0, 128, 16): u[r, h, h, 0] = 0.0 if r == o[0] else -1.0 if r == o[1] else 1.0
    w = layers(rng)
    w[:, :, :, :, :, 0] = 0
    return {"x": x.reshape(N, 128, 4 * C), "u": u.reshape(N, 128, 512), "v": d["v"], **weights(rng, w)}
def setup_inputs_near(rng):
    d = numbers_of(rng)
    x = d["x"].astype(np.float32).reshape(N, 8, 16, C, 4)
    u = d["u"].reshape(N, 128, 128, 4)
    h = rng.permutation(8)
    o = rng.permutation(N)
    x[:, :, 0] = 0
    x[:, :, 8:] = 0
    u[:, :, ::16] = 0
    for r in range(N):
        k = -1.0 if o[r] % 4 == 3 else 1.0
        for g in h[:4]:
            x[r, g, 0, :, 0] = np.where(rng.random(C) < rng.uniform(0.2, 0.9), 1.0, -1.0)
            s = rng.integers(0, 16 if o[r] % 2 else 8, C)
            x[r, g, 8] = ((s[:, None] >> np.arange(4)) & 1) * np.exp2(np.arange(4) - 23.0)
            x[r, g, 11, :, 0] = 2.0 ** -10
            a, m = 16 * int(g), k if o[r] < N // 2 else k * 2.0 ** -30
            u[r, a, a, 0] = m
            u[r, a + 8, a] = m
            u[r, a + 11, a, 0] = m
        for g in h[4:]:
            x[r, g, 10, :, 0] = (1.0 + 0.125 * rng.integers(0, 8, C)) * 2.0 ** -30
            u[r, 16 * int(g) + 10, 16 * int(g), 0] = k * 2.0 ** -30
        for g in h[6:]: x[r, g, 10, rng.integers(C), 0] = 2.0 ** 29
    w = layers(rng)
    w[:, :, 8:] = 0
    w[:, :, :, :, :, 8:] = 0
    w[:, :, 0] = 0
    w[:, :, :, :, :, 0] = 0
    return {"x": x.reshape(N, 128, 4 * C).astype(BF), "u": u.reshape(N, 128, 512), "v": d["v"], **weights(rng, w)}
def setup_inputs_huge(rng):
    d = numbers_of(rng)
    h = rng.permutation(8)
    o = rng.permutation(N)
    c = rng.integers(0, 2, 8) * 2.0 - 1.0
    x = (0.9 + 0.1 * rng.random((N, 8, 1, C, 1))) * (0.95 + 0.05 * rng.random((N, 8, 16, C, 4))) * c[:, None, None, None]
    x[:, h[4:]] *= rng.choice([-1.0, 1.0], (N, 4, 1, C, 1))
    u = d["u"].reshape(N, 128, 128, 4)
    for r in range(N):
        for g in range(8):
            a = 2.0 ** 30 * (1.0 - 0.1 * rng.random((8, 16, 4))) * c[:, None, None]
            if o[r] % 4 == 0: a = -a
            if o[r] % 4 < 2: a[h[4:]] = 0
            else: a[h[:4]] = 0
            u[r, :, 16 * g] = a.reshape(128, 4).astype(np.float32).astype(BF)
    w = np.zeros((N, 128, 4, 128, 4), np.float32)
    i = np.arange(128)
    for b in range(4): w[:, i, b, i, b] = -1
    return {"x": (2.0 ** 30 * x).astype(np.float32).reshape(N, 128, 4 * C).astype(BF), "u": u.reshape(N, 128, 512), "v": d["v"], **weights(rng, w.astype(BF))}
def setup_inputs_ends(rng):
    d = numbers_of(rng)
    x = d["x"].astype(np.float32).reshape(N, 8, 16, C, 4)
    h = rng.permutation(8)
    e = int(rng.integers(N))
    x[:, :, 0] = 0
    for g in range(8):
        p = rng.permutation(N)
        if g in h[:4]: p[(e + np.arange(N)) % N] = np.concatenate([[0, 1, N - 1, N - 2], 2 + rng.permutation(N - 4)])
        x[:, g, 0, :, 0] = np.exp2(p)[:, None] * (1.0 + 0.125 * rng.integers(0, 8, (N, C)))
    m = int(h[7])
    k = np.repeat(np.arange(4.0), [L // 4, L - L // 4, L, C - 2 * L])
    for r in range(N):
        j = rng.permutation(C)
        x[r, m, 0, j] = -np.exp2(k)[:, None]
        x[r, m, 0, j, r % 4] = np.exp2(4.0 - k)
        x[r, m, 0, j[C - 1], r % 4] = -1.5
    s = (N, 8, 8, C, 4)
    x[:, :, 8:] = rng.choice([-1.0, 1.0], s) * (1.0 + (2 * rng.integers(0, 64, s) + 1) * 0.0078125) * np.exp2(rng.integers(-14, -7, s))
    x[:, :, 8, :, 0] = rng.choice([-1.96875, 1.96875], (N, 8, C))
    u = d["u"].reshape(N, 128, 128, 4)
    u[:, :, ::16] = 0
    for a in range(0, 128, 16): u[:, a, a, 0] = 1
    for r in range(N):
        u[r, 16 * m, 16 * m, 0] = 0
        u[r, 16 * m, 16 * m, r % 4] = 1
    w = layers(rng)
    w[:, :, 0] = 0
    w[:, :, :, :, :, 0] = 0
    return {"x": x.reshape(N, 128, 4 * C).astype(BF), "u": u.reshape(N, 128, 512), "v": d["v"], **weights(rng, w)}
def setup_inputs_spread(rng):
    d = setup_inputs(rng)
    d["x"] = big(wide(rng, N, 128, 4 * C, cols=6))
    return d
def check_inputs(d):
    b = []
    for k in ("x", "u", "v"):
        a = np.abs(d[k].astype(np.float32))
        if not (np.isfinite(a).all() and ((a == 0) | (a >= 2.0 ** -30) & (a <= 2.0 ** 30)).all()): b.append("a value of " + k)
    none, least, most = [emit(mx_ref.quantize(np.full((128, 16), k, np.float32).astype(BF)))[1][0, 0] for k in (0.0, 2.0 ** -30, 2.0 ** 30)]
    for r in range(N):
        if ((d["wc"][r] == 0x7F) | (d["wc"][r] == 0xFF)).any(): b.append("wc: a code that is no number")
        s = mx_ref.live(d["ws"][r])
        if ((s != none) & ((s < least) | (s > most))).any(): b.append("ws: a scale out of range")
    return b
def reference(x, u, v, wc, ws):
    qu = [mx_ref.quantize(u[r]) for r in range(N)]
    lay = [pk(wc[r], ws[r]) for r in range(N)]
    now = [x[r] for r in range(N)]
    ls = np.zeros((N, 8, C + 2 * L), np.float32)
    for t in range(R):
        order, kept, gone = [], [], []
        for r in range(N):
            s = mx_ref.matmul(qu[r], mx_ref.quantize(now[r]))[::16] + np.float32(0.0)
            o = np.argsort(-s, axis=1, kind="stable")
            order.append(o)
            kept.append(np.take_along_axis(s, o[:, L:], axis=1))
            gone.append(mx_ref.quantize(gcols(now[r], o[:, :L])))
        came = [decode(gone[r]).astype(BF) for r in range(N)]
        final = []
        for r in range(N):
            said = []
            for e in ((r + 1) % N, (r + 2) % N):
                a = mx_ref.matmul(qu[e], gone[r])[::16] + np.float32(0.0)
                said.append(np.count_nonzero(kept[e][:, None, :] > a[:, :, None], axis=2))
            final.append(np.maximum(said[0], said[1]))
        made = []
        for r in range(N):
            lo, hi = sorted([(r - 1) % N, (r - 2) % N])
            place = np.concatenate([order[r][:, L:], np.tile(C + np.arange(2 * L), (8, 1))], axis=1)
            key = np.concatenate([np.tile(np.arange(C - L), (8, 1)), final[lo], final[hi]], axis=1)
            l = np.take_along_axis(place, np.argsort(key, axis=1, kind="stable")[:, :C], axis=1)
            ls[r] = np.concatenate([l, final[lo], final[hi]], axis=1)
            a = np.concatenate([now[r], came[lo], came[hi]], axis=1)
            before = np.concatenate([l[:, :1], l[:, :-1]], axis=1)
            z = ((gcols(a, l).astype(np.float32) + gcols(a, before).astype(np.float32)) * np.float32(0.5)).astype(BF)
            q = mx_ref.quantize(z)
            made.append(tile([mx_ref.matmul(pick(lay[r], np.arange(128 * b, 128 * b + 128)), q) * np.float32(0.03125) + z[:, b::4].astype(np.float32) for b in range(4)]))
        now = made
    y = np.zeros((N, 128, C), np.float32)
    oc, osc = np.zeros((N, 128, 4 * C), np.uint8), np.zeros((N, 16, C), np.uint8)
    for r in range(N):
        q = mx_ref.quantize(now[r])
        y[r] = mx_ref.matmul(mx_ref.quantize(v[r]), q)
        oc[r], osc[r] = emit(q)
    return {"y": y, "ls": ls, "oc": oc, "osc": osc}

@@ -1,0 +1,458 @@
+from concourse.bass import DstId, RemoteDMATransfer
+from concourse.mybir import dt, AluOpType, ActivationFunctionType
+
+ALU, ACT = AluOpType, ActivationFunctionType
+
+C, L, R = 320, 96, 3
+KEEP = C - L
+NS = 2 * L
+H = C // 2
+BIG = 1.0e29
+SM = 256.0
+F8 = "float8_e4m3fn_x4"
+TILES = [(0, 19, 18, 17), (16, 15, 14, 13), (12, 11, 10, 9), (8, 7, 6, 5), (4, 3, 2, 1)]
+TW = [320, 256, 192, 128, 128]
+TO = [0, 320, 576, 768, 896]
+NSS = 7
+NV = (12 - NSS) * NS
+POOLS = {"cf": ("float32", (("pf", 4), ("cola", 1), ("colg", 1), ("q16", C), ("q4", C), ("eq16", C), ("eq4", C), ("j192", NS), ("jg", 128),
+                            ("cst", 20), ("m16", C), ("m16n", KEEP), ("rs16", C), ("pat", NS), ("io1", NS), ("io2", NS), ("iod", 12))),
+         "af": ("float32", (("ff", NS), ("kk", NS), ("km", NS), ("kd", NS), ("fd", 12), ("hh", 12), ("acc", 12), ("p2", 12), ("lo", C))),
+         "ab": ("bfloat16", (("ww", NS + KEEP), ("flag", C), ("wm", C), ("wd", C), ("cum", C), ("cd", C), ("ld", C // 4), ("lf", C), ("lx", C),
+                             ("ly", C), ("ms", NV), ("mss", NV), ("junk2", NSS * NS)))}
+PART = {}
+
+
+def _scratch():
+    s = {}
+    def sb(name, n, d): s[name] = ("sbuf", [128, n], d)
+    bf, f32, i32, u16, u8 = "bfloat16", "float32", "int32", "uint16", "uint8"
+    for name, n in (("ut", 512), ("vt", 512), ("xt", 1280), ("x32", 1280), ("zt", 1280), ("z32", 1280), ("gt", 1280),
+                    ("at", 512), ("vw", 4 * (NS + KEEP)), ("ct", 4096), ("pt", 4 * NS), ("b1", 512), ("stmp", 2 * C), ("et", 2048),
+                    ("bt", 512), ("bt4", 512), ("xb", 48), ("yb", 48), ("r01", C), ("rds", C), ("jb", C), ("ow", C), ("m4b", C),
+                    ("rs4b", C), ("m16b", C), ("rs16b", C), ("xo", C), ("yo", C), ("xk", KEEP), ("yk", KEEP), ("junk", 3200),
+                    ("sid", NS), ("one5", 512), ("r192", NV)):
+        sb(name, n, bf)
+    for name, n in (("xs", C), ("ys", C), ("ss", C), ("sa", NS), ("sx", 16), ("sy", 16), ("rs", 20), ("w1", 20), ("w2", 20),
+                    ("rk", 20), ("kf", KEEP), ("ky", KEEP + 16), ("pks", NS), ("pl", NS + KEEP), ("yy", C)):
+        sb(name, n, f32)
+    for name in ("xc", "yc", "rs16h", "m16h"):
+        sb(name, C, "float16")
+    for pool, (d, parts) in POOLS.items():
+        at = 0
+        for name, n in parts:
+            PART[name] = (pool, at, n)
+            at += -(-n // 16) * 16
+        sb(pool, at, d)
+    for name, n in (("pi", 1), ("pj", 4), ("uo32", 8), ("qa", L), ("qi", NS)):
+        sb(name, n, i32)
+    for name, n in (("uo", 8), ("ofr", 20), ("ofa", 24), ("ofs", 56), ("ofk", 14), ("ofb", 12), ("ofp", 12), ("ofg", 80), ("ofl", 20)):
+        sb(name, n, u16)
+    for name, n in (("u0", 128), ("u1", 128), ("v", 128), ("x", C), ("z", C), ("w", 512), ("c", 1024), ("p", NS), ("o", 128),
+                    ("e", 512), ("b", 128), ("b4", 128)):
+        sb("q_" + name, n, F8)
+        sb("s_" + name, n, u8)
+    for t in range(R):
+        sb("q_a%d" % t, 128, F8); sb("s_a%d" % t, 128, u8)
+        sb("q_l%d" % t, NS, F8); sb("s_l%d" % t, NS, u8)
+        sb("pk%d" % t, L, u16); sb("pin%d" % t, L, u16)
+    for k in range(8):
+        s["ps%d" % k] = ("psum", [128, 512], f32)
+    return s
+
+
+SCRATCH = _scratch()
+NCS, NDS = 110, 24
+SEMAPHORES = (["c%d" % k for k in range(NCS)] + ["d%d" % k for k in range(NDS)] + ["loc"]
+              + ["arra%d" % t for t in range(R)] + ["arrp%d" % t for t in range(R)])
+
+
+def _meets(a, b):
+    if a[0] != b[0] or a[2] <= b[1] or b[2] <= a[1]:
+        return False
+    if a[3] == b[3] and a[3] > 1 and (a[1] - b[1]) % a[3]:
+        return False
+    return True
+
+
+def _emit(g, T, ops):
+    queue = {"V": g.vector, "S": g.scalar, "T": g.tensor, "G": g, "Y": g.sync}
+    known = {q: 0 for q in queue}
+    issued = {q: 0 for q in queue}
+    wanted = set()
+    for i, o in enumerate(ops):
+        deps = []
+        for j in range(i - 1, -1, -1):
+            p = ops[j]
+            if p["kind"] == "r" or known[o["q"]] >> j & 1:
+                continue
+            if p["q"] == "T" and o["q"] == "T":
+                continue
+            hit = any(_meets(a, b) for a in o["rd"] + o["wr"] for b in p["wr"]) or any(_meets(a, b) for a in o["wr"] for b in p["rd"])
+            if not hit and p["q"] != o["q"]:
+                hit = any(a[0] == b[0] and a[0].startswith("ps") for a in o["rd"] + o["wr"] for b in p["rd"] + p["wr"])
+            if hit:
+                deps.append(j)
+                known[o["q"]] |= p["known"] | (1 << j) | p["before"]
+        o["before"] = issued[o["q"]] if o["kind"] == "c" else 0
+        if o["kind"] == "c":
+            issued[o["q"]] |= 1 << i
+        o["deps"] = deps
+        o["known"] = known[o["q"]]
+        wanted.update(deps)
+    last, count, nd = {}, {}, [0]
+    tail = []
+    loc = 0
+    for i, o in enumerate(ops):
+        q = queue[o["q"]]
+        for j in o["deps"]:
+            q.wait_ge(T.sem[ops[j]["sem"]], ops[j]["val"])
+        for name, val in o["arr"]:
+            q.wait_ge(T.sem[name], val)
+        ins = o["fn"](q)
+        if o["kind"] == "r":
+            loc += o["loc"]
+        elif o["kind"] == "d":
+            name = "d%d" % nd[0]
+            nd[0] += 1
+            o["sem"], o["val"] = name, 16
+            ins.then_inc(T.sem[name], 16)
+            if i not in wanted:
+                tail.append(o)
+        elif i in wanted:
+            free = [k for k in range(NCS) if k not in last or o["known"] >> last[k] & 1]
+            k = min(free, key=lambda k: last.get(k, -1))
+            last[k] = i
+            count[k] = count.get(k, 0) + 1
+            o["sem"], o["val"] = "c%d" % k, count[k]
+            ins.then_inc(T.sem["c%d" % k], 1)
+    for o in tail:
+        queue[o["q"]].wait_ge(T.sem[o["sem"]], o["val"])
+    g.wait_ge(T.sem.loc, loc)
+
+
+def rank_program(g, core, T, topo):
+    rank = T.rank_of(core)
+    if rank is None:
+        return
+    n = len(T.cores)
+    ops = []
+
+    def senders(r): return sorted([(r - 1) % n, (r - 2) % n])
+
+    def A(name, lo=0, hi=None, step=1):
+        if name in PART:
+            pool, at, w = PART[name]
+            name, lo, hi = pool, at + lo, at + (w if hi is None else hi)
+        if hi is None: hi = T[name].shape[1]
+        return (T[name][:, lo:hi] if step == 1 else T[name][:, lo:hi:step], [(name, lo, hi, step)])
+
+    def IND(win, off):
+        return (win[0].indirect(off[0]), win[1] + off[1])
+
+    def op(q, fn, rd, wr, kind="c", arr=(), loc=0):
+        ops.append({"q": q, "fn": fn, "rd": [t for a in rd for t in a[1]], "wr": [t for a in wr for t in a[1]], "kind": kind, "arr": list(arr), "loc": loc})
+
+    def val(s): return s[0] if isinstance(s, tuple) else s
+    def aps(*s): return [a for a in s if isinstance(a, tuple)]
+
+    def memset(o, c): op("V", lambda q: q.memset(o[0], c), [], [o])
+    def copy(o, i, arr=()): op("V", lambda q: q.tensor_copy(o[0], i[0]), [i], [o], arr=arr)
+    def scatter(win, off, i): op("V", lambda q: q.tensor_copy(win[0].indirect(off[0]), i[0]), [i, off], [win])
+    def tt(o, a, b, f): op("V", lambda q: q.tensor_tensor(o[0], a[0], b[0], f), [a, b], [o])
+    def ts(o, a, s1, f1, s2=None, f2=None):
+        if f2 is None: op("V", lambda q: q.tensor_scalar(o[0], a[0], val(s1), None, f1), [a] + aps(s1), [o])
+        else: op("V", lambda q: q.tensor_scalar(o[0], a[0], val(s1), val(s2), f1, f2), [a] + aps(s1, s2), [o])
+    def scan(o, a, b, init, f0, f1): op("V", lambda q: q.tensor_tensor_scan(o[0], a[0], b[0], init, f0, f1), [a, b], [o])
+    def quant(name, lo, hi, i):
+        c, s = A("q_" + name, lo, hi), A("s_" + name, lo, hi)
+        op("V", lambda q: q.quantize_mx(c[0], s[0], i[0]), [i], [c, s])
+    def act(o, i, f, scale=1.0, bias=None, acc=None):
+        kw = {"scale": scale}
+        if bias is not None: kw["bias"] = bias[0]
+        if acc is not None: kw["accum_out"] = acc[0]
+        op("S", lambda q: q.activation(o[0], i[0], f, **kw), [i] + aps(bias), [o] + aps(acc))
+    def mm(bank, w, wlo, x, xlo, xhi, start=True, stop=True, arr=()):
+        o = A("ps%d" % bank, 0, xhi - xlo)
+        a, b, c, d = A("q_" + w, wlo, wlo + 128), A("s_" + w, wlo, wlo + 128), A("q_" + x, xlo, xhi), A("s_" + x, xlo, xhi)
+        op("T", lambda q: q.matmul_mx(o[0], a[0], b[0], c[0], d[0], start, stop), [a, b, c, d], [o], arr=arr)
+    def iota(o, pat, base, cm, small=True):
+        if small: op("G", lambda q: q.iota(o[0], pat, base, cm, allow_small_or_imprecise_dtypes=True), [], [o])
+        else: op("G", lambda q: q.iota(o[0], pat, base, cm), [], [o])
+    def unit_tile(b):
+        def call(q): return q.affine_select(T.et[:, 512 * b:512 * b + 512], T.one5[:], [[1, 512]], ALU.is_equal, 0.0, -b, -4)
+        op("G", call, [A("one5")], [A("et", 512 * b, 512 * b + 512)])
+    def dma(qn, o, i, rd, wr): op(qn, lambda q: q.dma_start(o, i), rd, wr, kind="d")
+    def PS(k, hi, lo=0): return A("ps%d" % k, lo, hi)
+    def rows(name): return T.af[0:128:16, PART[name][1]:PART[name][1] + PART[name][2]]
+    def to_diag(x, y, src, mask, reset, low, w):
+        tt(x, src, A(mask, 0, w), ALU.min)
+        scan(y, A(reset, 0, w), x, low, ALU.min, ALU.max)
+
+    def send(pieces, rd):
+        trs, tot = [], 0
+        for k, (d, src, dst, sem) in enumerate(pieces):
+            dc = T.cores[d]
+            eng = topo.engines(core, dc)
+            h = len(eng) // len(pieces)
+            mask = sum(1 << e for e in eng[k * h:(k + 1) * h])
+            rid, pid, _ = topo.addr(dc)
+            trs.append(RemoteDMATransfer(dst_ids=[DstId(rid=rid, pnc=pid)], dma_engine_mask=mask, remote_sem=T.sem[sem], src=src, dst=dst))
+            tot += h
+        op("G", lambda q: q.remote_dma_fused(trs, local_sem=T.sem.loc), rd, [], kind="r", loc=tot)
+
+    half = len(topo.engines(T.cores[senders(rank)[0]], core)) // 2
+
+    for h in range(2):
+        dma("Y", T.xt[:, 4 * H * h:4 * H * h + 4 * H], T.x[:, 4 * H * h:4 * H * h + 4 * H], [], [A("xt", 4 * H * h, 4 * H * h + 4 * H)])
+    dma("S", T.ut[:], T.u[:], [], [A("ut")])
+    dma("Y", T.q_w[:].bitcast(dt.uint8), T.wc[:], [], [A("q_w")])
+    dma("Y", T.s_w[:], T.ws[:], [], [A("s_w")])
+    dma("Y", T.vt[:], T.v[:], [], [A("vt")])
+
+    iota(A("pi"), [[0, 1]], 0, 1, False)
+    iota(A("uo32"), [[16, 8]], 0, 0, False)
+    iota(A("q16"), [[0, 20], [1, 16]], 0, 0)
+    iota(A("cst"), [[16, 20]], 15, 0)
+    iota(A("q4"), [[0, 80], [1, 4]], 0, 0)
+    iota(A("jg"), [[1, 8], [0, 16]], 0, 0)
+    iota(A("jb"), [[1, C]], -128, 0)
+    iota(A("bt4"), [[0, 512]], 0, 0)
+    iota(A("pat"), [[0, L], [256, 2]], 0, 0)
+    iota(A("pt", 2, 4 * NS, 4), [[0, NS]], 0, 0)
+    iota(A("pt", 3, 4 * NS, 4), [[0, NS]], 0, 0)
+    iota(A("b1", NS, 512), [[0, 512 - NS]], 0, 0)
+    iota(A("j192"), [[1, NS]], 0, 0)
+    iota(A("one5"), [[0, 512]], 1, 0)
+    unit_tile(0)
+    unit_tile(1)
+    memset(A("rs16"), BIG)
+    for m in range(5):
+        memset(A("ct", 4 * TO[m] + 64 * TILES[m][3], 4 * (TO[m] + TW[m])), 0.0)
+    ts(A("pj", 0, 1), A("pi"), 15, ALU.bitwise_and)
+    ts(A("pj", 1, 2), A("pi"), 3, ALU.bitwise_and)
+    ts(A("pj", 2, 3), A("pi"), 2, ALU.logical_shift_right, 3, ALU.bitwise_and)
+    ts(A("pj", 3, 4), A("pi"), 4, ALU.logical_shift_right)
+    memset(A("rs16", 0, C, 16), -BIG)
+    copy(A("uo"), A("uo32"))
+    copy(A("pf"), A("pj"))
+    pr, p4, pe, pg = [A("pf", k, k + 1) for k in range(4)]
+    memset(A("r01"), 1.0)
+    ts(A("eq16"), A("q16"), pr, ALU.is_equal, 0.5, ALU.subtract)
+    act(A("m16"), A("eq16"), ACT.Copy, scale=2 * BIG)
+    act(A("rs16h"), A("rs16"), ACT.Copy, scale=1024 / BIG)
+    act(A("m16h"), A("eq16"), ACT.Copy, scale=2048.0)
+    memset(A("rs4b"), SM)
+    memset(A("r01", 0, C, 16), 0.0)
+    memset(A("rs", 0, 1), 0.0)
+    memset(A("at", 4 * L, 512), 0.0)
+    memset(A("rs4b", 0, C, 4), -SM)
+    ts(A("cst"), A("cst"), pr, ALU.subtract)
+    memset(A("ow"), 0.0)
+    ts(A("cola"), p4, float(C), ALU.mult, 128.0, ALU.add)
+    ts(A("eq4"), A("q4"), pe, ALU.is_equal, 0.5, ALU.subtract)
+    act(A("m4b"), A("eq4"), ACT.Copy, scale=2 * SM)
+    quant("u0", 0, 128, A("ut"))
+    uw = (T.q_u0[:, 0:128].bitcast(dt.uint32).indirect(T.uo[:, 0:8]), A("q_u0")[1] + A("uo")[1])
+    op("V", lambda q: q.tensor_copy(T.q_u1[:, 0:128].bitcast(dt.uint32), uw[0]), [uw], [A("q_u1")])
+    copy(A("s_u1"), IND(A("s_u0"), A("uo")))
+
+    def quant_x(h, w):
+        quant("x", H * h, H * h + H, A("xt", 4 * H * h, 4 * H * h + 4 * H))
+        mm(4 + 2 * h, w, 0, "x", H * h, H * h + H)
+        if w == "u1":
+            mm(5 + 2 * h, w, 0, "x", H * h, H * h + H)
+            act(A("ss", H * h, H * h + H), PS(5 + 2 * h, H), ACT.Copy)
+
+    quant_x(0, "u1")
+    quant_x(1, "u1")
+    for b in range(4):
+        ts(A("bt", b, 512, 4), A("jg"), pg, ALU.is_equal)
+
+    mine = senders(rank)
+    for t in range(R):
+        lastr = t == R - 1
+        for h in range(2):
+            tt(A("xs", H * h, H * h + H), PS(4 + 2 * h, H), A("m16", 0, H), ALU.min)
+        scan(A("ys"), A("rs16"), A("xs"), -BIG, ALU.min, ALU.max)
+        def col(c): return A("ys", 16 * c + 15, 16 * c + 16)
+        for e in (1, 2):
+            c = TILES[0][e]
+            act(A("stmp", C * (e - 1), C * (e - 1) + 16 * c), A("ss", 0, 16 * c), ACT.Sign, scale=-1.0, bias=col(c))
+        for e in (1, 2):
+            c = TILES[0][e]
+            act(A("ct", e, 64 * c, 4), A("stmp", C * (e - 1), C * (e - 1) + 16 * c), ACT.Relu, acc=A("rs", c, c + 1))
+        jo = 0
+        for m in range(5):
+            base = 4 * TO[m]
+            for e, c in enumerate(TILES[m]):
+                if c == 0:
+                    for h in range(2):
+                        tt(A("ct", 4 * H * h, 4 * H * h + 4 * H, 4), A("ys", H * h, H * h + H), PS(4 + 2 * h, H), ALU.is_ge)
+                elif m or e == 3:
+                    ts(A("ct", base + e, base + 64 * c, 4), A("ss", 0, 16 * c), col(c), ALU.is_lt)
+                    act(A("junk", jo, jo + 16 * c), A("ct", base + e, base + 64 * c, 4), ACT.Identity, acc=A("rs", c, c + 1))
+                    jo += 16 * c
+            if m == 1 and t == 0:
+                quant("b", 0, 128, A("bt"))
+            if m > 0:
+                quant("c", TO[m - 1], TO[m - 1] + TW[m - 1], A("ct", 4 * TO[m - 1], 4 * (TO[m - 1] + TW[m - 1])))
+                mm(2, "b", 0, "c", TO[m - 1], TO[m - 1] + TW[m - 1], m == 1, False)
+        quant("c", TO[4], TO[4] + TW[4], A("ct", 4 * TO[4], 4 * (TO[4] + TW[4])))
+        mm(2, "b", 0, "c", TO[4], TO[4] + TW[4], False, True)
+        scan(A("rds"), A("r01"), A("ct", 0, 4 * C, 4), 0.0, ALU.mult, ALU.add)
+        if t == 0:
+            for b in range(4):
+                act(A("x32", C * b, C * b + C), A("xt", b, 4 * C, 4), ACT.Copy, scale=32.0)
+            act(A("m16b"), A("eq16"), ACT.Copy, scale=2 * SM)
+            act(A("rs16b"), A("rs16"), ACT.Copy, scale=SM / BIG)
+            act(A("m16n"), A("eq16", 0, KEEP), ACT.Copy, scale=-2 * BIG)
+        tt(A("w1"), A("cst"), A("rds", 15, C, 16), ALU.subtract)
+        tt(A("xc"), PS(2, C), A("m16h"), ALU.min)
+        tt(A("w2"), A("w1"), A("rs"), ALU.subtract)
+        scan(A("yc"), A("rs16h"), A("xc"), -1024.0, ALU.min, ALU.max)
+        tt(A("rk"), A("yc", 15, C, 16), A("w2"), ALU.add)
+        copy(A("ofr"), A("rk"))
+        scatter(A("ow"), A("ofr"), A("jb"))
+        to_diag(A("xo", 0, L), A("yo", 0, L), A("ow", 0, L), "m4b", "rs4b", -SM, L)
+        ts(A("ofa"), A("yo", 3, L, 4), A("cola"), ALU.add)
+        act(A("at", 192, 384), IND(A("x32"), A("ofa", 12, 24)), ACT.Copy, scale=1.0 / 32)
+        ts(A("at", 0, 192), IND(A("x32"), A("ofa", 0, 12)), 1.0 / 32, ALU.mult)
+        an, ln = "a%d" % t, "l%d" % t
+        quant(an, 0, 128, A("at"))
+        to = [(rank + 1) % n, (rank + 2) % n]
+        at = [L * senders(d).index(rank) for d in to]
+        send([(d, T["q_" + an][:, 0:L].bitcast(dt.uint8), T["q_" + ln][:, a:a + L].bitcast(dt.uint8), "arra%d" % t) for d, a in zip(to, at)], [A("q_" + an)])
+        send([(d, T["s_" + an][:, 0:L], T["s_" + ln][:, a:a + L], "arra%d" % t) for d, a in zip(to, at)], [A("s_" + an)])
+        if t == 0:
+            unit_tile(2)
+            unit_tile(3)
+        tt(A("xk"), A("ow", L, C), A("m16b", 0, KEEP), ALU.min)
+        tt(A("xo", L, C), A("ow", L, C), A("m4b", 0, KEEP), ALU.min)
+        scan(A("yk"), A("rs16b", 0, KEEP), A("xk"), -SM, ALU.min, ALU.max)
+        scan(A("yo", L, C), A("rs4b", 0, KEEP), A("xo", L, C), -SM, ALU.min, ALU.max)
+        ts(A("ofk"), A("yk", 15, KEEP, 16), 128.0, ALU.add)
+        ts(A("ofs"), A("yo", L + 3, C, 4), A("cola"), ALU.add)
+        act(A("vw", 4 * NS, 4 * (NS + KEEP)), IND(A("x32"), A("ofs")), ACT.Copy, scale=1.0 / 64)
+        copy(A("kf"), IND(A("ss"), A("ofk")))
+        if t == 0:
+            memset(A("ky", KEEP, KEEP + 16), -BIG)
+            for b in range(4):
+                ts(A("bt4", 5 * b, 512, 16), A("jg", b, 128, 4), pg, ALU.is_equal)
+        tt(A("sx", 0, 14), A("kf", 15, KEEP, 16), A("m16", 0, 14), ALU.min)
+        scan(A("ky", 0, KEEP), A("m16n"), A("kf"), -BIG, ALU.min, ALU.max)
+        scan(A("sy", 0, 14), A("rs16", 0, 14), A("sx", 0, 14), -BIG, ALU.min, ALU.max)
+        if t == 0:
+            quant("b4", 0, 128, A("bt4"))
+        mm(0, "u1", 0, ln, 0, NS, arr=[("arra%d" % t, 4 * half)])
+        mm(1, "u1", 0, ln, 0, NS)
+        act(A("sa"), PS(1, NS), ACT.Copy)
+        ts(A("b1", 0, NS), PS(0, NS), A("sy", 13, 14), ALU.is_lt)
+        quant("o", 0, 128, A("b1"))
+        mm(2, "b4", 0, "o", 0, 128)
+        ts(A("pt", 1, 4 * NS, 4), PS(0, NS), A("sy", 13, 14), ALU.is_lt, 16.0, ALU.mult)
+        to_diag(A("xb"), A("yb"), PS(2, NS // 4), "m4b", "rs4b", -SM, NS // 4)
+        ts(A("ofb"), A("yb", 3, NS // 4, 4), 16.0, ALU.mult, 15.0, ALU.add)
+        tt(A("pt", 0, 4 * NS, 4), IND(A("ky"), A("ofb")), A("sa"), ALU.is_gt)
+        quant("p", 0, NS, A("pt"))
+        mm(3, "b", 0, "p", 0, NS)
+        scan(A("pks"), A("pat"), PS(3, NS), 0.0, ALU.mult, ALU.add)
+        copy(A("pk%d" % t), A("pks", 1, NS, 2))
+        pieces = []
+        for k, s in enumerate(mine):
+            d = [r for r in ((s + 1) % n, (s + 2) % n) if r != rank][0]
+            a = (L // 2) * senders(d).index(s)
+            pieces.append((d, T["pk%d" % t][:, (L // 2) * k:(L // 2) * (k + 1)], T["pin%d" % t][:, a:a + L // 2], "arrp%d" % t))
+        send(pieces, [A("pk%d" % t)])
+        memset(A("ww"), SM)
+        for b in range(4):
+            if t == 0:
+                quant("e", 128 * b, 128 * b + 128, A("et", 512 * b, 512 * b + 512))
+            mm(4 + b, "e", 128 * b, ln, 0, NS)
+            act(A("vw", b, 4 * NS, 4), PS(4 + b, NS), ACT.Copy, scale=0.5)
+        if t == 0:
+            ts(A("io1"), A("j192"), 1.0 / 256, ALU.mult)
+            ts(A("sid"), A("j192"), -float(NS), ALU.add)
+            ts(A("iod"), A("j192", 0, NS, 16), pr, ALU.add, 1.0 / 256, ALU.mult)
+            ts(A("colg"), p4, float(4 * NS), ALU.add)
+            memset(A("r192"), 1.0)
+            tt(A("io2"), A("io1"), A("m16", 0, NS), ALU.min)
+            memset(A("r192", 0, NV, NS), 0.0)
+        if t == 1:
+            quant("v", 0, 128, A("vt"))
+        if lastr:
+            ts(A("pl", 0, NS), A("j192"), float(C), ALU.add)
+            ts(A("pl", NS, NS + KEEP), A("ow", L, C), 128.0, ALU.add)
+        copy(A("qa"), A("pin%d" % t), arr=[("arrp%d" % t, 2 * half)])
+        ts(A("qi", 0, NS, 2), A("qa"), 8, ALU.logical_shift_right)
+        ts(A("qi", 1, NS, 2), A("qa"), 255, ALU.bitwise_and)
+        tt(A("ff"), A("qi"), PS(3, NS), ALU.max)
+        tt(A("km"), A("ff"), A("io2"), ALU.add)
+        tt(A("kk"), A("ff"), A("io1"), ALU.add)
+        scan(A("kd"), A("rs16", 0, NS), A("km"), -BIG, ALU.min, ALU.max)
+        if lastr:
+            dma("Y", T.ls[:, C:C + NS], rows("ff"), [A("ff")], [])
+        def key(c): return A("kd", 16 * c + 15, 16 * c + 16)
+        for c in range(NSS):
+            act(A("junk2", NS * c, NS * c + NS), A("kk"), ACT.Sign, scale=-1.0, bias=key(c), acc=A("acc", c, c + 1))
+        tt(A("fd"), A("kd", 15, NS, 16), A("iod"), ALU.subtract)
+        for c in range(NSS, 12):
+            ts(A("ms", NS * (c - NSS), NS * (c - NSS + 1)), A("kk"), key(c), ALU.is_lt, 2.0, ALU.mult)
+        ts(A("hh"), A("fd"), float(KEEP - 1), ALU.min, 2.0, ALU.mult)
+        scan(A("mss"), A("r192"), A("ms"), 0.0, ALU.mult, ALU.add)
+        tt(A("p2", 0, NSS), A("acc", 0, NSS), A("hh", 0, NSS), ALU.add)
+        tt(A("p2", NSS, 12), A("mss", NS - 1, NV, NS), A("hh", NSS, 12), ALU.add)
+        ts(A("ofp", 0, NSS), A("p2", 0, NSS), 0.5, ALU.mult, 1.0 + (NS - 1) / 2, ALU.add)
+        ts(A("ofp", NSS, 12), A("p2", NSS, 12), 0.5, ALU.mult, 1.0, ALU.add)
+        scatter(A("ww"), A("ofp"), A("sid"))
+        ts(A("flag"), A("ww", 0, C), 0.0, ALU.is_gt)
+        tt(A("wm"), A("ww", 0, C), A("m4b"), ALU.min)
+        scan(A("cum"), A("one5", 0, C), A("flag"), -1.0, ALU.mult, ALU.add)
+        scan(A("wd"), A("rs4b"), A("wm"), -SM, ALU.min, ALU.max)
+        scan(A("cd"), A("m4b"), A("cum"), -SM, ALU.max, ALU.min)
+        if lastr: tt(A("lf"), A("ww", 0, C), A("cum"), ALU.min)
+        tt(A("ld"), A("wd", 3, C, 4), A("cd", 3, C, 4), ALU.min)
+        if lastr: tt(A("lx"), A("lf"), A("m16b"), ALU.min)
+        ts(A("ofg"), A("ld"), 4.0, ALU.mult, A("colg"), ALU.add)
+        if lastr: scan(A("ly"), A("rs16b"), A("lx"), -SM, ALU.min, ALU.max)
+        for k in range(1, 4):
+            act(A("gt", C * k, C * k + C), IND(A("vw"), A("ofg", 20 * k, 20 * k + 20)), ACT.Copy)
+        copy(A("gt", 0, C), IND(A("vw"), A("ofg", 0, 20)))
+        if lastr: ts(A("ofl"), A("ly", 15, C, 16), float(NS), ALU.add)
+        tt(A("zt", 4, C), A("gt", 4, C), A("gt", 0, C - 4), ALU.add)
+        ts(A("zt", 0, 4), A("gt", 0, 4), 2.0, ALU.mult)
+        banks = [[4, 5, 6, 7], [0, 1, 2, 3]]
+        for k in range(1, 4):
+            tt(A("zt", C * k, C * k + C), A("gt", C * k, C * k + C), A("gt", C * k - 4, C * k + C - 4), ALU.add)
+            if k == 2 or k == 3:
+                h = k - 2
+                quant("z", H * h, H * h + H, A("zt", 4 * H * h, 4 * H * h + 4 * H))
+                for b in range(4):
+                    mm(banks[h][b], "w", 128 * b, "z", H * h, H * h + H)
+        for h in range(2):
+            for b in range(4):
+                act(A("z32", C * b + H * h, C * b + H * h + H), A("zt", 4 * H * h + b, 4 * H * h + 4 * H, 4), ACT.Copy, scale=32.0)
+        def part(name, h, b): return A(name, C * b + H * h, C * b + H * h + H)
+        def xpart(h, b): return A("xt", 4 * H * h + b, 4 * H * h + 4 * H, 4)
+        for b in range(4):
+            tt(part("x32", 0, b), PS(banks[0][b], H), part("z32", 0, b), ALU.add)
+        for b in range(4):
+            act(xpart(0, b), part("x32", 0, b), ACT.Copy, scale=1.0 / 32)
+        if lastr:
+            act(A("lo"), IND(A("pl"), A("ofl")), ACT.Copy)
+            dma("Y", T.ls[:, 0:C], rows("lo"), [A("lo")], [])
+        for b in range(4):
+            tt(part("x32", 1, b), PS(banks[1][b], H), part("z32", 1, b), ALU.add)
+            if b > 0:
+                ts(xpart(1, b - 1), part("x32", 1, b - 1), 1.0 / 32, ALU.mult)
+        quant_x(0, "v" if lastr else "u1")
+        ts(xpart(1, 3), part("x32", 1, 3), 1.0 / 32, ALU.mult)
+        quant_x(1, "v" if lastr else "u1")
+
+    for h in range(2):
+        dma("Y", T.oc[:, 4 * H * h:4 * H * h + 4 * H], T.q_x[:, H * h:H * h + H].bitcast(dt.uint8), [A("q_x", H * h, H * h + H)], [])
+        act(A("yy", H * h, H * h + H), PS(4 + 2 * h, H), ACT.Copy)
+        dma("S", T.y[:, H * h:H * h + H], T.yy[:, H * h:H * h + H], [A("yy", H * h, H * h + H)], [])
+    for k in range(4):
+        dma("Y", T.osc[4 * k:4 * k + 4, :], T.s_x[32 * k:32 * k + 4, :], [A("s_x")], [])
+    _emit(g, T, ops)

@@ -1,5 +1,5 @@
 from concourse.bass import DstId, RemoteDMATransfer
-from concourse.mybir import dt, AluOpType, ActivationFunctionType
+from concourse.mybir import dt, AluOpType, ActivationFunctionType, AxisListType
 
 ALU, ACT = AluOpType, ActivationFunctionType
 
@@ -7,19 +7,32 @@ C, L, R = 320, 96, 3
 KEEP = C - L
 NS = 2 * L
 H = C // 2
-BIG = 1.0e29
-SM = 256.0
+BIG = 1.0e25
+SM = 2048
+STAY = 200
+TINY = 2.0 ** -19
 F8 = "float8_e4m3fn_x4"
 TILES = [(0, 19, 18, 17), (16, 15, 14, 13), (12, 11, 10, 9), (8, 7, 6, 5), (4, 3, 2, 1)]
 TW = [320, 256, 192, 128, 128]
 TO = [0, 320, 576, 768, 896]
+S_ONLY = (9, 8, 7, 13, 12)
+V_SUM = (4, 3, 2, 1)
 NSS = 7
-NV = (12 - NSS) * NS
-POOLS = {"cf": ("float32", (("pf", 4), ("cola", 1), ("colg", 1), ("q16", C), ("q4", C), ("eq16", C), ("eq4", C), ("j192", NS), ("jg", 128),
-                            ("cst", 20), ("m16", C), ("m16n", KEEP), ("rs16", C), ("pat", NS), ("io1", NS), ("io2", NS), ("iod", 12))),
-         "af": ("float32", (("ff", NS), ("kk", NS), ("km", NS), ("kd", NS), ("fd", 12), ("hh", 12), ("acc", 12), ("p2", 12), ("lo", C))),
-         "ab": ("bfloat16", (("ww", NS + KEEP), ("flag", C), ("wm", C), ("wd", C), ("cum", C), ("cd", C), ("ld", C // 4), ("lf", C), ("lx", C),
-                             ("ly", C), ("ms", NV), ("mss", NV), ("junk2", NSS * NS)))}
+MW = NS + 2
+B1 = NS + 32
+TB = NS + B1
+GV = [(0, 12), (12, 24)]
+GS = [(24, 40), (40, 60), (60, 80)]
+SD = 2
+POOLS = {"cf": ("float32", (("pf", 4), ("cola", 1), ("colr", 1), ("cl", 1), ("c2", 1), ("j192", NS), ("jg", 128),
+                            ("m16", H), ("m16n", KEEP), ("rs16", H), ("iod", 16), ("ge", 128))),
+         "cb": ("bfloat16", (("sid", NS), ("k4", C), ("k16", C), ("q16", C), ("q4", C), ("eq16", C), ("ramp", 256), ("rsd", C), ("m16h", C),
+                             ("jb", C), ("m4b", C), ("rs4b", C), ("m16b", C), ("rs16b", C), ("rmw", 12 * MW), ("r16", TB))),
+         "af": ("float32", (("f32", NS), ("kk", NS), ("kd", 16), ("acc", 12), ("p2", 12), ("hl", 1), ("lo", C))),
+         "ab": ("bfloat16", (("b1", 2 * B1), ("t1", 2 * TB), ("s1", 2 * TB), ("s16", 24), ("b2", 2 * NS), ("t2", 2 * NS), ("s2", 2 * NS),
+                             ("tot", 32), ("fo", NS), ("fw", TB), ("ffp", B1), ("ww", NS + KEEP), ("wm", C),
+                             ("lx", C), ("junk2", 12 * NS), ("ms", 16 * MW), ("mss", 12 * MW))),
+         "ah": ("float16", (("cum", C), ("wx", C), ("wy", C), ("lf", C), ("ly", C)))}
 PART = {}
 
 
@@ -27,35 +40,35 @@ def _scratch():
     s = {}
     def sb(name, n, d): s[name] = ("sbuf", [128, n], d)
     bf, f32, i32, u16, u8 = "bfloat16", "float32", "int32", "uint16", "uint8"
-    for name, n in (("ut", 512), ("vt", 512), ("xt", 1280), ("x32", 1280), ("zt", 1280), ("z32", 1280), ("gt", 1280),
-                    ("at", 512), ("vw", 4 * (NS + KEEP)), ("ct", 4096), ("pt", 4 * NS), ("b1", 512), ("stmp", 2 * C), ("et", 2048),
-                    ("bt", 512), ("bt4", 512), ("xb", 48), ("yb", 48), ("r01", C), ("rds", C), ("jb", C), ("ow", C), ("m4b", C),
-                    ("rs4b", C), ("m16b", C), ("rs16b", C), ("xo", C), ("yo", C), ("xk", KEEP), ("yk", KEEP), ("junk", 3200),
-                    ("sid", NS), ("one5", 512), ("r192", NV)):
+    for name, n in (("ut", 512), ("vt", 512), ("xt", 1280), ("x32", 1280), ("zt", 1280), ("z32", 1280), ("gt", 1296),
+                    ("at", 512), ("vw", 4 * (STAY + KEEP)), ("ct", 4096), ("stmp", 6 * C), ("et", 2048),
+                    ("bt", 512), ("xc", C), ("yc", C), ("rds", C), ("ow", C),
+                    ("xo", C), ("yo", C), ("xk", KEEP), ("yk", KEEP), ("junk", 3200), ("one5", 512)):
         sb(name, n, bf)
-    for name, n in (("xs", C), ("ys", C), ("ss", C), ("sa", NS), ("sx", 16), ("sy", 16), ("rs", 20), ("w1", 20), ("w2", 20),
-                    ("rk", 20), ("kf", KEEP), ("ky", KEEP + 16), ("pks", NS), ("pl", NS + KEEP), ("yy", C)):
+    for name, n in (("xs", C), ("ys", C), ("ss", C), ("sa", 2 * NS), ("sx", 16), ("rs", 20), ("w2", 20),
+                    ("rk", 20), ("kf", KEEP), ("ky", KEEP), ("pl", STAY + KEEP), ("yy", C)):
         sb(name, n, f32)
-    for name in ("xc", "yc", "rs16h", "m16h"):
-        sb(name, C, "float16")
+    for name, n in (("lev", NS), ("lev1", 2 * NS)):
+        sb(name, n, "float16")
     for pool, (d, parts) in POOLS.items():
         at = 0
         for name, n in parts:
             PART[name] = (pool, at, n)
             at += -(-n // 16) * 16
         sb(pool, at, d)
-    for name, n in (("pi", 1), ("pj", 4), ("uo32", 8), ("qa", L), ("qi", NS)):
+    for name, n in (("pi", 1), ("pj", 4), ("uo32", 12), ("pk", 4)):
         sb(name, n, i32)
-    for name, n in (("uo", 8), ("ofr", 20), ("ofa", 24), ("ofs", 56), ("ofk", 14), ("ofb", 12), ("ofp", 12), ("ofg", 80), ("ofl", 20)):
+    for name, n in (("uo", 8), ("un", 12), ("u8", 2), ("lp", 2), ("ofr", 20), ("ofa", 24), ("ofs", 56), ("ofk", 14), ("ofb", 32),
+                    ("ofp", 12), ("ofg", 80), ("ofl", 20)):
         sb(name, n, u16)
-    for name, n in (("u0", 128), ("u1", 128), ("v", 128), ("x", C), ("z", C), ("w", 512), ("c", 1024), ("p", NS), ("o", 128),
-                    ("e", 512), ("b", 128), ("b4", 128)):
+    for name, n in (("u0", 128), ("u1", 128), ("u2", 16), ("ul", 64), ("uf", 256), ("v", 128), ("x", C), ("z", C), ("w", 512),
+                    ("c", 1024), ("e", 512), ("b", 128)):
         sb("q_" + name, n, F8)
         sb("s_" + name, n, u8)
     for t in range(R):
         sb("q_a%d" % t, 128, F8); sb("s_a%d" % t, 128, u8)
         sb("q_l%d" % t, NS, F8); sb("s_l%d" % t, NS, u8)
-        sb("pk%d" % t, L, u16); sb("pin%d" % t, L, u16)
+        sb("km%d" % t, 16, f32); sb("kin%d" % t, 32, f32)
     for k in range(8):
         s["ps%d" % k] = ("psum", [128, 512], f32)
     return s
@@ -63,7 +76,7 @@ def _scratch():
 
 SCRATCH = _scratch()
 NCS, NDS = 110, 24
-SEMAPHORES = (["c%d" % k for k in range(NCS)] + ["d%d" % k for k in range(NDS)] + ["loc"]
+SEMAPHORES = (["c%d" % k for k in range(NCS)] + ["d%d" % k for k in range(NDS)] + ["loc", "arru"]
               + ["arra%d" % t for t in range(R)] + ["arrp%d" % t for t in range(R)])
 
 
@@ -157,19 +170,25 @@ def rank_program(g, core, T, topo):
     def aps(*s): return [a for a in s if isinstance(a, tuple)]
 
     def memset(o, c): op("V", lambda q: q.memset(o[0], c), [], [o])
-    def copy(o, i, arr=()): op("V", lambda q: q.tensor_copy(o[0], i[0]), [i], [o], arr=arr)
+    def copy(o, i): op("V", lambda q: q.tensor_copy(o[0], i[0]), [i], [o])
     def scatter(win, off, i): op("V", lambda q: q.tensor_copy(win[0].indirect(off[0]), i[0]), [i, off], [win])
     def tt(o, a, b, f): op("V", lambda q: q.tensor_tensor(o[0], a[0], b[0], f), [a, b], [o])
-    def ts(o, a, s1, f1, s2=None, f2=None):
-        if f2 is None: op("V", lambda q: q.tensor_scalar(o[0], a[0], val(s1), None, f1), [a] + aps(s1), [o])
-        else: op("V", lambda q: q.tensor_scalar(o[0], a[0], val(s1), val(s2), f1, f2), [a] + aps(s1, s2), [o])
-    def scan(o, a, b, init, f0, f1): op("V", lambda q: q.tensor_tensor_scan(o[0], a[0], b[0], init, f0, f1), [a, b], [o])
+    def ts(o, a, s1, f1, s2=None, f2=None, arr=()):
+        if f2 is None: op("V", lambda q: q.tensor_scalar(o[0], a[0], val(s1), None, f1), [a] + aps(s1), [o], arr=arr)
+        else: op("V", lambda q: q.tensor_scalar(o[0], a[0], val(s1), val(s2), f1, f2), [a] + aps(s1, s2), [o], arr=arr)
+    def scan(o, a, b, init, f0, f1): op("V", lambda q: q.tensor_tensor_scan(o[0], a[0], b[0], float(init), f0, f1), [a, b], [o])
+    def reduce(o, i, f): op("V", lambda q: q.tensor_reduce(o[0], i[0], AxisListType.X, f), [i], [o])
+    def turn(o, i): op("V", lambda q: q.transpose(o[0], i[0]), [i], [o])
+    def pick(to, lo, hi, frm, a, b, off, arr=()):
+        o, w = A("q_" + to, lo, hi), A("q_" + frm, a, b)
+        op("V", lambda q: q.tensor_copy(o[0].bitcast(dt.uint32), w[0].bitcast(dt.uint32).indirect(off[0])), [w, off], [o], arr=arr)
+        copy(A("s_" + to, lo, hi), IND(A("s_" + frm, a, b), off))
     def quant(name, lo, hi, i):
         c, s = A("q_" + name, lo, hi), A("s_" + name, lo, hi)
         op("V", lambda q: q.quantize_mx(c[0], s[0], i[0]), [i], [c, s])
     def act(o, i, f, scale=1.0, bias=None, acc=None):
         kw = {"scale": scale}
-        if bias is not None: kw["bias"] = bias[0]
+        if bias is not None: kw["bias"] = val(bias)
         if acc is not None: kw["accum_out"] = acc[0]
         op("S", lambda q: q.activation(o[0], i[0], f, **kw), [i] + aps(bias), [o] + aps(acc))
     def mm(bank, w, wlo, x, xlo, xhi, start=True, stop=True, arr=()):
@@ -185,9 +204,8 @@ def rank_program(g, core, T, topo):
     def dma(qn, o, i, rd, wr): op(qn, lambda q: q.dma_start(o, i), rd, wr, kind="d")
     def PS(k, hi, lo=0): return A("ps%d" % k, lo, hi)
     def rows(name): return T.af[0:128:16, PART[name][1]:PART[name][1] + PART[name][2]]
-    def to_diag(x, y, src, mask, reset, low, w):
-        tt(x, src, A(mask, 0, w), ALU.min)
-        scan(y, A(reset, 0, w), x, low, ALU.min, ALU.max)
+    def mask(x, src, m): scan(x, src, m, -SM, ALU.max, ALU.min)
+    def hold(y, x, reset, low=-SM): scan(y, reset, x, low, ALU.min, ALU.max)
 
     def send(pieces, rd):
         trs, tot = [], 0
@@ -195,264 +213,317 @@ def rank_program(g, core, T, topo):
             dc = T.cores[d]
             eng = topo.engines(core, dc)
             h = len(eng) // len(pieces)
-            mask = sum(1 << e for e in eng[k * h:(k + 1) * h])
+            m = sum(1 << e for e in eng[k * h:(k + 1) * h])
             rid, pid, _ = topo.addr(dc)
-            trs.append(RemoteDMATransfer(dst_ids=[DstId(rid=rid, pnc=pid)], dma_engine_mask=mask, remote_sem=T.sem[sem], src=src, dst=dst))
+            trs.append(RemoteDMATransfer(dst_ids=[DstId(rid=rid, pnc=pid)], dma_engine_mask=m, remote_sem=T.sem[sem], src=src, dst=dst))
             tot += h
         op("G", lambda q: q.remote_dma_fused(trs, local_sem=T.sem.loc), rd, [], kind="r", loc=tot)
 
     half = len(topo.engines(T.cores[senders(rank)[0]], core)) // 2
 
+    dma("S", T.ut[:], T.u[:], [], [A("ut")])
     for h in range(2):
         dma("Y", T.xt[:, 4 * H * h:4 * H * h + 4 * H], T.x[:, 4 * H * h:4 * H * h + 4 * H], [], [A("xt", 4 * H * h, 4 * H * h + 4 * H)])
-    dma("S", T.ut[:], T.u[:], [], [A("ut")])
-    dma("Y", T.q_w[:].bitcast(dt.uint8), T.wc[:], [], [A("q_w")])
+    dma("Y", T.q_w[:].bitcast(dt.uint8), T.wc[:], [A("xt")], [A("q_w")])
     dma("Y", T.s_w[:], T.ws[:], [], [A("s_w")])
     dma("Y", T.vt[:], T.v[:], [], [A("vt")])
 
     iota(A("pi"), [[0, 1]], 0, 1, False)
-    iota(A("uo32"), [[16, 8]], 0, 0, False)
+    iota(A("uo32"), [[1, 12]], 0, 0, False)
     iota(A("q16"), [[0, 20], [1, 16]], 0, 0)
-    iota(A("cst"), [[16, 20]], 15, 0)
-    iota(A("q4"), [[0, 80], [1, 4]], 0, 0)
+    iota(A("rs16b"), [[0, 20], [2 * SM, 16]], -SM, 0)
     iota(A("jg"), [[1, 8], [0, 16]], 0, 0)
+    iota(A("rsd"), [[-16, 20], [2 * SM, 16]], 128, 0)
     iota(A("jb"), [[1, C]], -128, 0)
-    iota(A("bt4"), [[0, 512]], 0, 0)
-    iota(A("pat"), [[0, L], [256, 2]], 0, 0)
-    iota(A("pt", 2, 4 * NS, 4), [[0, NS]], 0, 0)
-    iota(A("pt", 3, 4 * NS, 4), [[0, NS]], 0, 0)
-    iota(A("b1", NS, 512), [[0, 512 - NS]], 0, 0)
-    iota(A("j192"), [[1, NS]], 0, 0)
-    iota(A("one5"), [[0, 512]], 1, 0)
-    unit_tile(0)
-    unit_tile(1)
-    memset(A("rs16"), BIG)
+    memset(A("one5"), 1.0)
+    memset(A("ow"), 0.0)
+    memset(A("at", 4 * L, 512), 0.0)
+    memset(A("r16"), 1.0 * SM)
+    memset(A("rs4b"), 1.0 * SM)
     for m in range(5):
         memset(A("ct", 4 * TO[m] + 64 * TILES[m][3], 4 * (TO[m] + TW[m])), 0.0)
+    memset(A("b1"), 0.0)
+    memset(A("ffp"), 0.0)
+    memset(A("r16", 0, TB, 16), 0.0)
+    memset(A("rs4b", 0, C, 4), -1.0 * SM)
     ts(A("pj", 0, 1), A("pi"), 15, ALU.bitwise_and)
     ts(A("pj", 1, 2), A("pi"), 3, ALU.bitwise_and)
     ts(A("pj", 2, 3), A("pi"), 2, ALU.logical_shift_right, 3, ALU.bitwise_and)
     ts(A("pj", 3, 4), A("pi"), 4, ALU.logical_shift_right)
-    memset(A("rs16", 0, C, 16), -BIG)
-    copy(A("uo"), A("uo32"))
+    ts(A("pk", 0, 1), A("pi"), 7, ALU.bitwise_and)
+    ts(A("uo"), A("uo32", 0, 8), 16.0, ALU.mult)
+    quant("u0", 0, 128, A("ut"))
     copy(A("pf"), A("pj"))
     pr, p4, pe, pg = [A("pf", k, k + 1) for k in range(4)]
-    memset(A("r01"), 1.0)
-    ts(A("eq16"), A("q16"), pr, ALU.is_equal, 0.5, ALU.subtract)
-    act(A("m16"), A("eq16"), ACT.Copy, scale=2 * BIG)
-    act(A("rs16h"), A("rs16"), ACT.Copy, scale=1024 / BIG)
-    act(A("m16h"), A("eq16"), ACT.Copy, scale=2048.0)
-    memset(A("rs4b"), SM)
-    memset(A("r01", 0, C, 16), 0.0)
     memset(A("rs", 0, 1), 0.0)
-    memset(A("at", 4 * L, 512), 0.0)
-    memset(A("rs4b", 0, C, 4), -SM)
-    ts(A("cst"), A("cst"), pr, ALU.subtract)
-    memset(A("ow"), 0.0)
-    ts(A("cola"), p4, float(C), ALU.mult, 128.0, ALU.add)
-    ts(A("eq4"), A("q4"), pe, ALU.is_equal, 0.5, ALU.subtract)
-    act(A("m4b"), A("eq4"), ACT.Copy, scale=2 * SM)
-    quant("u0", 0, 128, A("ut"))
-    uw = (T.q_u0[:, 0:128].bitcast(dt.uint32).indirect(T.uo[:, 0:8]), A("q_u0")[1] + A("uo")[1])
-    op("V", lambda q: q.tensor_copy(T.q_u1[:, 0:128].bitcast(dt.uint32), uw[0]), [uw], [A("q_u1")])
-    copy(A("s_u1"), IND(A("s_u0"), A("uo")))
+    ts(A("u8", 0, 1), A("pk", 0, 1), 16.0, ALU.mult)
+    copy(A("un"), A("uo32"))
+    memset(A("ms", NS + 1, 12 * MW, MW), -2.0 * KEEP)
+    pick("u1", 0, 128, "u0", 0, 128, A("uo"))
+    mine = senders(rank)
+    other = [[r for r in ((s + 1) % n, (s + 2) % n) if r != rank][0] for s in mine]
+    place = [senders(d).index(s) for d, s in zip(other, mine)]
+    pick("u2", 0, 16, "u0", 0, 128, A("u8", 0, 1))
+    send([(d, T.q_u2[:, 0:16].bitcast(dt.uint8), T.q_ul[:, 32 * a:32 * a + 16].bitcast(dt.uint8), "arru") for d, a in zip(other, place)], [A("q_u2")])
+    send([(d, T.s_u2[:, 0:16], T.s_ul[:, 32 * a:32 * a + 16], "arru") for d, a in zip(other, place)], [A("s_u2")])
+    iota(A("q4"), [[0, 80], [1, 4]], 0, 0)
+    iota(A("j192"), [[1, NS]], 1, 0)
+    iota(A("ramp"), [[16, 16], [0, 16]], 0, 0)
+    for b in range(2): unit_tile(b)
+    ts(A("eq16"), A("q16"), pr, ALU.is_equal, 0.5, ALU.subtract)
+    act(A("m16"), A("eq16", 0, H), ACT.Copy, scale=2 * BIG)
+    act(A("rs16"), A("rs16b", 0, H), ACT.Copy, scale=BIG / SM)
 
-    def quant_x(h, w):
+    def col(c): return A("ys", 16 * c + 15, 16 * c + 16)
+    def lane(c):
+        m = [k for k in range(5) if c in TILES[k]][0]
+        return A("ct", 4 * TO[m] + TILES[m].index(c), 4 * TO[m] + 64 * c, 4)
+    def strip(c):
+        if c in S_ONLY:
+            k = C * S_ONLY.index(c)
+            act(A("stmp", k, k + 16 * c), A("ss", 0, 16 * c), ACT.Sign, scale=-1.0, bias=col(c))
+        else:
+            ts(lane(c), A("ss", 0, 16 * c), col(c), ALU.is_lt)
+    def strip_sum(c):
+        if c in S_ONLY:
+            k = C * S_ONLY.index(c)
+            act(lane(c), A("stmp", k, k + 16 * c), ACT.Relu, acc=A("rs", c, c + 1))
+        elif c in V_SUM:
+            reduce(A("rs", c, c + 1), lane(c), ALU.add)
+        else:
+            act(A("junk", 8 * c * (c - 1), 8 * c * (c + 1)), lane(c), ACT.Identity, acc=A("rs", c, c + 1))
+    def quant_c(m): quant("c", TO[m], TO[m] + TW[m], A("ct", 4 * TO[m], 4 * (TO[m] + TW[m])))
+    def sum_c(m, start=False, stop=False): mm(2, "b", 0, "c", TO[m], TO[m] + TW[m], start, stop)
+    def shared(m): return [c for c in TILES[m] if c and c not in S_ONLY]
+    def scores(h, w):
         quant("x", H * h, H * h + H, A("xt", 4 * H * h, 4 * H * h + 4 * H))
         mm(4 + 2 * h, w, 0, "x", H * h, H * h + H)
-        if w == "u1":
-            mm(5 + 2 * h, w, 0, "x", H * h, H * h + H)
-            act(A("ss", H * h, H * h + H), PS(5 + 2 * h, H), ACT.Copy)
+        if w == "u1": mm(5 + 2 * h, w, 0, "x", H * h, H * h + H)
+    def quant_e(b): quant("e", 128 * b, 128 * b + 128, A("et", 512 * b, 512 * b + 512))
 
-    quant_x(0, "u1")
-    quant_x(1, "u1")
+    scores(0, "u1")
+    ts(A("ge"), A("jg"), pg, ALU.is_equal)
     for b in range(4):
-        ts(A("bt", b, 512, 4), A("jg"), pg, ALU.is_equal)
-
-    mine = senders(rank)
+        act(A("bt", b, 512, 4), A("ge"), ACT.Copy)
+    memset(A("rmw", MW * NSS), 1.0)
     for t in range(R):
         lastr = t == R - 1
-        for h in range(2):
-            tt(A("xs", H * h, H * h + H), PS(4 + 2 * h, H), A("m16", 0, H), ALU.min)
-        scan(A("ys"), A("rs16"), A("xs"), -BIG, ALU.min, ALU.max)
-        def col(c): return A("ys", 16 * c + 15, 16 * c + 16)
-        for e in (1, 2):
-            c = TILES[0][e]
-            act(A("stmp", C * (e - 1), C * (e - 1) + 16 * c), A("ss", 0, 16 * c), ACT.Sign, scale=-1.0, bias=col(c))
-        for e in (1, 2):
-            c = TILES[0][e]
-            act(A("ct", e, 64 * c, 4), A("stmp", C * (e - 1), C * (e - 1) + 16 * c), ACT.Relu, acc=A("rs", c, c + 1))
-        jo = 0
-        for m in range(5):
-            base = 4 * TO[m]
-            for e, c in enumerate(TILES[m]):
-                if c == 0:
-                    for h in range(2):
-                        tt(A("ct", 4 * H * h, 4 * H * h + 4 * H, 4), A("ys", H * h, H * h + H), PS(4 + 2 * h, H), ALU.is_ge)
-                elif m or e == 3:
-                    ts(A("ct", base + e, base + 64 * c, 4), A("ss", 0, 16 * c), col(c), ALU.is_lt)
-                    act(A("junk", jo, jo + 16 * c), A("ct", base + e, base + 64 * c, 4), ACT.Identity, acc=A("rs", c, c + 1))
-                    jo += 16 * c
-            if m == 1 and t == 0:
-                quant("b", 0, 128, A("bt"))
-            if m > 0:
-                quant("c", TO[m - 1], TO[m - 1] + TW[m - 1], A("ct", 4 * TO[m - 1], 4 * (TO[m - 1] + TW[m - 1])))
-                mm(2, "b", 0, "c", TO[m - 1], TO[m - 1] + TW[m - 1], m == 1, False)
-        quant("c", TO[4], TO[4] + TW[4], A("ct", 4 * TO[4], 4 * (TO[4] + TW[4])))
-        mm(2, "b", 0, "c", TO[4], TO[4] + TW[4], False, True)
-        scan(A("rds"), A("r01"), A("ct", 0, 4 * C, 4), 0.0, ALU.mult, ALU.add)
+        act(A("ss", 0, H), PS(5, H), ACT.Copy)
+        tt(A("xs", 0, H), PS(4, H), A("m16", 0, H), ALU.min)
+        scores(1, "u1")
+        act(A("ss", H, C), PS(7, H), ACT.Copy)
+        hold(A("ys", 0, H), A("xs", 0, H), A("rs16", 0, H), -BIG)
         if t == 0:
-            for b in range(4):
-                act(A("x32", C * b, C * b + C), A("xt", b, 4 * C, 4), ACT.Copy, scale=32.0)
-            act(A("m16b"), A("eq16"), ACT.Copy, scale=2 * SM)
-            act(A("rs16b"), A("rs16"), ACT.Copy, scale=SM / BIG)
-            act(A("m16n"), A("eq16", 0, KEEP), ACT.Copy, scale=-2 * BIG)
-        tt(A("w1"), A("cst"), A("rds", 15, C, 16), ALU.subtract)
-        tt(A("xc"), PS(2, C), A("m16h"), ALU.min)
-        tt(A("w2"), A("w1"), A("rs"), ALU.subtract)
-        scan(A("yc"), A("rs16h"), A("xc"), -1024.0, ALU.min, ALU.max)
-        tt(A("rk"), A("yc", 15, C, 16), A("w2"), ALU.add)
-        copy(A("ofr"), A("rk"))
+            memset(A("rmw", 0, 12 * MW, MW), 0.0)
+            ts(A("cola"), p4, 512.0, ALU.add)
+            ts(A("colr"), pr, -1.0, ALU.mult, 15.0 + 256, ALU.add)
+            memset(A("vw", 0, 4), 0.0)
+            memset(A("vw", 4 + 4 * NS, 4 * STAY), 0.0)
+            memset(A("pl", 0, 1), 0.0)
+            memset(A("pl", NS + 1, STAY), 0.0)
+        tt(A("xs", H, C), PS(6, H), A("m16", 0, H), ALU.min)
+        first = [c for c in S_ONLY if 16 * c + 16 <= H]
+        for c in first: strip(c)
+        for c in first: strip_sum(c)
+        tt(A("ct", 0, 4 * H, 4), A("ys", 0, H), PS(4, H), ALU.is_ge)
+        hold(A("ys", H, C), A("xs", H, C), A("rs16", 0, H), -BIG)
+        for c in shared(4): strip(c)
+        rest = [c for c in S_ONLY if c not in first]
+        for c in rest: strip(c)
+        for c in rest: strip_sum(c)
+        tt(A("ct", 4 * H, 4 * C, 4), A("ys", H, C), PS(6, H), ALU.is_ge)
+        for m in range(4):
+            for k, c in enumerate(shared(m)):
+                strip(c)
+                strip_sum(c)
+                if m == 0 and k == 0: quant_c(4)
+                if m == 0 and k == 1 and t == 0: quant("b", 0, 128, A("bt"))
+                if m and k == 0:
+                    quant_c(m - 1)
+                    sum_c(m - 1, start=m == 1)
+                    if m == 1: sum_c(4)
+        if t == 0:
+            ts(A("m16h"), A("eq16"), 2.0 * SM, ALU.mult, -128.0 - SM, ALU.add)
+        scan(A("rds"), A("rsd"), A("ct", 0, 4 * C, 4), SM, ALU.min, ALU.add)
+        quant_c(3)
+        sum_c(3, stop=True)
+        for c in shared(4): strip_sum(c)
+        if t == 0:
+            act(A("q4"), A("q4"), ACT.Abs, scale=-1.0, bias=pe)
+            act(A("m16b"), A("eq16"), ACT.Copy, scale=2.0 * SM)
+            act(A("m4b"), A("q4"), ACT.Identity, scale=-2.0 * SM, bias=1.0 * SM)
+        tt(A("xc"), PS(2, C), A("m16h"), ALU.add)
+        tt(A("w2"), A("rds", 15, C, 16), A("rs"), ALU.add)
+        hold(A("yc"), A("xc"), A("rs16b"))
+        if t == 0:
+            tt(A("pk", 1, 2), A("pj", 0, 1), A("pj", 3, 4), ALU.add)
+            for k in range(R): memset(A("km%d" % k, 14, 15), -BIG)
+        tt(A("rk"), A("yc", 15, C, 16), A("w2"), ALU.subtract)
+        if t == 0: quant_e(0)
+        ts(A("ofr"), A("rk"), A("colr"), ALU.add)
+        if t == 0: ts(A("pk", 2, 3), A("pk", 1, 2), 1, ALU.bitwise_and)
         scatter(A("ow"), A("ofr"), A("jb"))
-        to_diag(A("xo", 0, L), A("yo", 0, L), A("ow", 0, L), "m4b", "rs4b", -SM, L)
-        ts(A("ofa"), A("yo", 3, L, 4), A("cola"), ALU.add)
-        act(A("at", 192, 384), IND(A("x32"), A("ofa", 12, 24)), ACT.Copy, scale=1.0 / 32)
-        ts(A("at", 0, 192), IND(A("x32"), A("ofa", 0, 12)), 1.0 / 32, ALU.mult)
-        an, ln = "a%d" % t, "l%d" % t
+        mask(A("xo", 0, L), A("ow", 0, L), A("m4b", 0, L))
+        mask(A("xk"), A("ow", L, C), A("m16b", 0, KEEP))
+        hold(A("yo", 0, L), A("xo", 0, L), A("rs4b", 0, L))
+        mask(A("xo", L, C), A("ow", L, C), A("m4b", 0, KEEP))
+        ts(A("ofa"), A("yo", 3, L, 4), 4.0, ALU.mult, A("cola"), ALU.add)
+        hold(A("yk"), A("xk"), A("rs16b", 0, KEEP))
+        act(A("at", 192, 384), IND(A("xt"), A("ofa", 12, 24)), ACT.Copy)
+        copy(A("at", 0, 192), IND(A("xt"), A("ofa", 0, 12)))
+        hold(A("yo", L, C), A("xo", L, C), A("rs4b", 0, KEEP))
+        ts(A("ofk"), A("yk", 15, KEEP, 16), 128.0, ALU.add)
+        an, ln, km, kin = "a%d" % t, "l%d" % t, "km%d" % t, "kin%d" % t
         quant(an, 0, 128, A("at"))
         to = [(rank + 1) % n, (rank + 2) % n]
         at = [L * senders(d).index(rank) for d in to]
         send([(d, T["q_" + an][:, 0:L].bitcast(dt.uint8), T["q_" + ln][:, a:a + L].bitcast(dt.uint8), "arra%d" % t) for d, a in zip(to, at)], [A("q_" + an)])
         send([(d, T["s_" + an][:, 0:L], T["s_" + ln][:, a:a + L], "arra%d" % t) for d, a in zip(to, at)], [A("s_" + an)])
-        if t == 0:
-            unit_tile(2)
-            unit_tile(3)
-        tt(A("xk"), A("ow", L, C), A("m16b", 0, KEEP), ALU.min)
-        tt(A("xo", L, C), A("ow", L, C), A("m4b", 0, KEEP), ALU.min)
-        scan(A("yk"), A("rs16b", 0, KEEP), A("xk"), -SM, ALU.min, ALU.max)
-        scan(A("yo", L, C), A("rs4b", 0, KEEP), A("xo", L, C), -SM, ALU.min, ALU.max)
-        ts(A("ofk"), A("yk", 15, KEEP, 16), 128.0, ALU.add)
-        ts(A("ofs"), A("yo", L + 3, C, 4), A("cola"), ALU.add)
-        act(A("vw", 4 * NS, 4 * (NS + KEEP)), IND(A("x32"), A("ofs")), ACT.Copy, scale=1.0 / 64)
+        ts(A("ofs"), A("yo", L + 3, C, 4), 4.0, ALU.mult, A("cola"), ALU.add)
         copy(A("kf"), IND(A("ss"), A("ofk")))
         if t == 0:
-            memset(A("ky", KEEP, KEEP + 16), -BIG)
-            for b in range(4):
-                ts(A("bt4", 5 * b, 512, 16), A("jg", b, 128, 4), pg, ALU.is_equal)
+            act(A("m16n"), A("eq16", 0, KEEP), ACT.Copy, scale=-2 * BIG)
+            quant_e(1)
+        act(A("vw", 4 * STAY, 4 * (STAY + KEEP)), IND(A("xt"), A("ofs")), ACT.Copy, scale=0.5)
         tt(A("sx", 0, 14), A("kf", 15, KEEP, 16), A("m16", 0, 14), ALU.min)
-        scan(A("ky", 0, KEEP), A("m16n"), A("kf"), -BIG, ALU.min, ALU.max)
-        scan(A("sy", 0, 14), A("rs16", 0, 14), A("sx", 0, 14), -BIG, ALU.min, ALU.max)
+        scan(A("ky"), A("m16n"), A("kf"), -BIG, ALU.min, ALU.max)
+        reduce(A(km, 15, 16), A("sx", 0, 14), ALU.max)
+        copy(A(km, 0, 14), A("ky", 15, KEEP, 16))
+        send([(d, T[km][:, 0:16], T[kin][:, 16 * a:16 * a + 16], "arrp%d" % t) for d, a in zip(other, place)], [A(km)])
+        memset(A("ww"), 1.0)
         if t == 0:
-            quant("b4", 0, 128, A("bt4"))
-        mm(0, "u1", 0, ln, 0, NS, arr=[("arra%d" % t, 4 * half)])
-        mm(1, "u1", 0, ln, 0, NS)
-        act(A("sa"), PS(1, NS), ACT.Copy)
-        ts(A("b1", 0, NS), PS(0, NS), A("sy", 13, 14), ALU.is_lt)
-        quant("o", 0, 128, A("b1"))
-        mm(2, "b4", 0, "o", 0, 128)
-        ts(A("pt", 1, 4 * NS, 4), PS(0, NS), A("sy", 13, 14), ALU.is_lt, 16.0, ALU.mult)
-        to_diag(A("xb"), A("yb"), PS(2, NS // 4), "m4b", "rs4b", -SM, NS // 4)
-        ts(A("ofb"), A("yb", 3, NS // 4, 4), 16.0, ALU.mult, 15.0, ALU.add)
-        tt(A("pt", 0, 4 * NS, 4), IND(A("ky"), A("ofb")), A("sa"), ALU.is_gt)
-        quant("p", 0, NS, A("pt"))
-        mm(3, "b", 0, "p", 0, NS)
-        scan(A("pks"), A("pat"), PS(3, NS), 0.0, ALU.mult, ALU.add)
-        copy(A("pk%d" % t), A("pks", 1, NS, 2))
-        pieces = []
-        for k, s in enumerate(mine):
-            d = [r for r in ((s + 1) % n, (s + 2) % n) if r != rank][0]
-            a = (L // 2) * senders(d).index(s)
-            pieces.append((d, T["pk%d" % t][:, (L // 2) * k:(L // 2) * (k + 1)], T["pin%d" % t][:, a:a + L // 2], "arrp%d" % t))
-        send(pieces, [A("pk%d" % t)])
-        memset(A("ww"), SM)
-        for b in range(4):
-            if t == 0:
-                quant("e", 128 * b, 128 * b + 128, A("et", 512 * b, 512 * b + 512))
-            mm(4 + b, "e", 128 * b, ln, 0, NS)
-            act(A("vw", b, 4 * NS, 4), PS(4 + b, NS), ACT.Copy, scale=0.5)
-        if t == 0:
-            ts(A("io1"), A("j192"), 1.0 / 256, ALU.mult)
-            ts(A("sid"), A("j192"), -float(NS), ALU.add)
-            ts(A("iod"), A("j192", 0, NS, 16), pr, ALU.add, 1.0 / 256, ALU.mult)
-            ts(A("colg"), p4, float(4 * NS), ALU.add)
-            memset(A("r192"), 1.0)
-            tt(A("io2"), A("io1"), A("m16", 0, NS), ALU.min)
-            memset(A("r192", 0, NV, NS), 0.0)
+            for b in range(2, 4): unit_tile(b)
+            for a in range(2): pick("uf", 128 * a, 128 * a + 128, "ul", 32 * a, 32 * a + 16, A("un", 0, 8), arr=[("arru", 4 * half)])
+            ts(A("cl"), A("pk", 2, 3), NS + 16.0, ALU.mult, 15.0, ALU.add)
+            ts(A("c2"), pr, 11.0, ALU.min, 16.0, ALU.mult)
+            ts(A("lev1", 0, NS), A("q16", 0, NS), pr, ALU.is_gt, 1.0 / 16, ALU.mult)
+            ts(A("lev1", NS), A("ramp", 0, NS), 1.0 / 256, ALU.mult, -KEEP / 2, ALU.add)
+            ts(A("lp", 0, 1), A("c2"), A("cl"), ALU.add)
+            tt(A("lev"), A("lev1", 0, NS), A("lev1", NS), ALU.add)
+            ts(A("iod"), A("ramp", 0, 256, 16), 1.0 / 256, ALU.mult, 1.0 / 32 - KEEP / 2, ALU.add)
         if t == 1:
             quant("v", 0, 128, A("vt"))
+        copy(A("gt", 0, 4), A("vw", 4 * STAY, 4 * STAY + 4))
+        def unpack(b):
+            mm(4 + b, "e", 128 * b, ln, 0, NS)
+            act(A("vw", 4 + b, 4 + 4 * NS, 4), PS(4 + b, NS), ACT.Copy, scale=0.5)
+        mm(0, "u1", 0, ln, 0, NS, arr=[("arra%d" % t, 4 * half)])
+        mm(1, "uf", 0, ln, 0, 128)
+        mm(2, "uf", 128, ln, NS - 128, NS)
+        views = [[(PS(0, NS), 0, NS, km, 0)], [(PS(1, L), 0, L, kin, 0), (PS(2, 128, 128 - L), L, NS, kin, 16)]]
+        def runs(e):
+            for s, lo, hi, w, a in views[e]:
+                ts(A("b1", B1 * e + 16 + lo, B1 * e + 16 + hi), s, A(w, a + 15, a + 16), ALU.is_lt, arr=[("arrp%d" % t, 2 * half)] if e and not lo else ())
+                act(A("sa", NS * e + lo, NS * e + hi), s, ACT.Copy)
+        def turns(e):
+            turn(A("t1", TB * e, TB * e + NS), A("b1", B1 * e + 16, B1 * e + 16 + NS))
+            turn(A("t1", TB * e + NS, TB * e + TB), A("b1", B1 * e, B1 * e + B1))
+        def sums(e):
+            for lo, hi in ((0, NS), (NS, TB)):
+                scan(A("s1", TB * e + lo, TB * e + hi), A("r16", lo, hi), A("t1", TB * e + lo, TB * e + hi), 0.0, ALU.min, ALU.add)
+        def lists(e):
+            ts(A("s16", 12 * e, 12 * e + 12), A("s1", TB * e + 15, TB * e + NS, 16), 16.0, ALU.mult)
+            copy(A("ofb", 16 * e, 16 * e + 16), IND(A("s1", TB * e, TB * e + TB), A("lp", 0, 1)))
+        def places(e):
+            for s, lo, hi, w, a in views[e]:
+                tt(A("b2", NS * e + lo, NS * e + hi), IND(A(w, a, a + 16), A("ofb", 16 * e + lo // 16, 16 * e + hi // 16)),
+                   A("sa", NS * e + lo, NS * e + hi), ALU.is_gt)
+        def turn2(e): turn(A("t2", NS * e, NS * e + NS), A("b2", NS * e, NS * e + NS))
+        def sum2(e): scan(A("s2", NS * e, NS * e + NS), A("r16", 0, NS), A("t2", NS * e, NS * e + NS), 0.0, ALU.min, ALU.add)
+        def total(e): tt(A("tot", 16 * e, 16 * e + 12), A("s2", NS * e + 15, NS * e + NS, 16), A("s16", 12 * e, 12 * e + 12), ALU.add)
+        steps = [runs, turns, sums, lists, places]
+        runs(0)
+        for k in range(1, 5):
+            steps[k](0)
+            steps[k - 1](1)
+            if k == 1:
+                for b in range(4 if t else 2): unpack(b)
+        if t == 0:
+            act(A("k4"), A("m4b"), ACT.Relu, scale=1 / (TINY * SM))
+            act(A("sid"), A("j192"), ACT.Copy, scale=TINY)
+            for b in range(2, 4):
+                quant_e(b)
+                unpack(b)
+        if t == 1:
+            act(A("k16"), A("m16b"), ACT.Relu, scale=1 / (TINY * SM))
+            act(A("pl", 1, NS + 1), A("j192"), ACT.Identity, bias=C - 1.0)
         if lastr:
-            ts(A("pl", 0, NS), A("j192"), float(C), ALU.add)
-            ts(A("pl", NS, NS + KEEP), A("ow", L, C), 128.0, ALU.add)
-        copy(A("qa"), A("pin%d" % t), arr=[("arrp%d" % t, 2 * half)])
-        ts(A("qi", 0, NS, 2), A("qa"), 8, ALU.logical_shift_right)
-        ts(A("qi", 1, NS, 2), A("qa"), 255, ALU.bitwise_and)
-        tt(A("ff"), A("qi"), PS(3, NS), ALU.max)
-        tt(A("km"), A("ff"), A("io2"), ALU.add)
-        tt(A("kk"), A("ff"), A("io1"), ALU.add)
-        scan(A("kd"), A("rs16", 0, NS), A("km"), -BIG, ALU.min, ALU.max)
-        if lastr:
-            dma("Y", T.ls[:, C:C + NS], rows("ff"), [A("ff")], [])
-        def key(c): return A("kd", 16 * c + 15, 16 * c + 16)
+            act(A("pl", STAY, STAY + KEEP), A("ow", L, C), ACT.Identity, bias=128.0)
+        turn2(0)
+        places(1)
+        sum2(0)
+        turn2(1)
+        total(0)
+        sum2(1)
+        copy(A("fo"), IND(A("tot", 0, 12), A("un")))
+        total(1)
+        tt(A("fw", 0, NS), IND(A("tot", 16, 28), A("un")), A("fo"), ALU.max)
+        ff = A("ffp", 16, 16 + NS)
+        turn(ff, A("fw", 0, NS))
+        turn(A("fw", NS, TB), A("ffp"))
+        tt(A("kk"), ff, A("lev"), ALU.add)
+        fd = IND(A("fw"), A("lp", 0, 1))
+        tt(A("kd"), fd, A("iod"), ALU.add)
+        def key(c): return A("kd", c, c + 1)
         for c in range(NSS):
             act(A("junk2", NS * c, NS * c + NS), A("kk"), ACT.Sign, scale=-1.0, bias=key(c), acc=A("acc", c, c + 1))
-        tt(A("fd"), A("kd", 15, NS, 16), A("iod"), ALU.subtract)
+        if lastr:
+            act(A("f32"), ff, ACT.Copy)
+            dma("Y", T.ls[:, C:C + NS], rows("f32"), [A("f32")], [])
+        ts(A("ms", NS, 16 * MW, MW), fd, float(KEEP - 1), ALU.min, 2.0, ALU.mult)
         for c in range(NSS, 12):
-            ts(A("ms", NS * (c - NSS), NS * (c - NSS + 1)), A("kk"), key(c), ALU.is_lt, 2.0, ALU.mult)
-        ts(A("hh"), A("fd"), float(KEEP - 1), ALU.min, 2.0, ALU.mult)
-        scan(A("mss"), A("r192"), A("ms"), 0.0, ALU.mult, ALU.add)
-        tt(A("p2", 0, NSS), A("acc", 0, NSS), A("hh", 0, NSS), ALU.add)
-        tt(A("p2", NSS, 12), A("mss", NS - 1, NV, NS), A("hh", NSS, 12), ALU.add)
-        ts(A("ofp", 0, NSS), A("p2", 0, NSS), 0.5, ALU.mult, 1.0 + (NS - 1) / 2, ALU.add)
-        ts(A("ofp", NSS, 12), A("p2", NSS, 12), 0.5, ALU.mult, 1.0, ALU.add)
+            ts(A("ms", MW * c, MW * c + NS), A("kk"), key(c), ALU.is_lt, 2.0, ALU.mult)
+        for lo, hi in ((NSS, 10), (10, 12)):
+            scan(A("mss", MW * lo, MW * hi), A("rmw", MW * lo, MW * hi), A("ms", MW * lo, MW * hi), 0.0, ALU.mult, ALU.add)
+        e = NSS - 1
+        ts(A("hl"), A("ms", MW * e + NS, MW * e + NS + 1), 0.5, ALU.mult, NS / 2, ALU.add)
+        tt(A("p2", 0, e), A("acc", 0, e), A("ms", NS, MW * e, MW), ALU.add)
+        ts(A("ofp", NSS, 12), A("mss", MW * NSS + MW - 1, 12 * MW, MW), 0.5, ALU.mult, 1.0 * KEEP, ALU.add)
+        ts(A("ofp", 0, e), A("p2", 0, e), 0.5, ALU.mult, NS / 2, ALU.add)
+        ts(A("ofp", e, NSS), A("acc", e, NSS), 0.5, ALU.mult, A("hl"), ALU.add)
         scatter(A("ww"), A("ofp"), A("sid"))
-        ts(A("flag"), A("ww", 0, C), 0.0, ALU.is_gt)
-        tt(A("wm"), A("ww", 0, C), A("m4b"), ALU.min)
-        scan(A("cum"), A("one5", 0, C), A("flag"), -1.0, ALU.mult, ALU.add)
-        scan(A("wd"), A("rs4b"), A("wm"), -SM, ALU.min, ALU.max)
-        scan(A("cd"), A("m4b"), A("cum"), -SM, ALU.max, ALU.min)
-        if lastr: tt(A("lf"), A("ww", 0, C), A("cum"), ALU.min)
-        tt(A("ld"), A("wd", 3, C, 4), A("cd", 3, C, 4), ALU.min)
-        if lastr: tt(A("lx"), A("lf"), A("m16b"), ALU.min)
-        ts(A("ofg"), A("ld"), 4.0, ALU.mult, A("colg"), ALU.add)
-        if lastr: scan(A("ly"), A("rs16b"), A("lx"), -SM, ALU.min, ALU.max)
-        for k in range(1, 4):
-            act(A("gt", C * k, C * k + C), IND(A("vw"), A("ofg", 20 * k, 20 * k + 20)), ACT.Copy)
-        copy(A("gt", 0, C), IND(A("vw"), A("ofg", 0, 20)))
-        if lastr: ts(A("ofl"), A("ly", 15, C, 16), float(NS), ALU.add)
-        tt(A("zt", 4, C), A("gt", 4, C), A("gt", 0, C - 4), ALU.add)
-        ts(A("zt", 0, 4), A("gt", 0, 4), 2.0, ALU.mult)
+        scan(A("cum"), A("one5", 0, C), A("ww", 0, C), STAY - 1, ALU.mult, ALU.add)
+        tt(A("wm"), A("ww", 0, C), A("k4"), ALU.mult)
+        scan(A("wx"), A("cum"), A("wm"), -SM, ALU.max, ALU.min)
+        hold(A("wy"), A("wx"), A("rs4b"))
+        ts(A("ofg"), A("wy", 3, C, 4), 4.0, ALU.mult, p4, ALU.add)
+        def gathered(lo, hi): return A("gt", 16 * lo + 4, 16 * hi + 4), IND(A("vw"), A("ofg", lo, hi))
+        def add(lo, hi): tt(A("zt", 16 * lo, 16 * hi), A("gt", 16 * lo + 4, 16 * hi + 4), A("gt", 16 * lo, 16 * hi), ALU.add)
         banks = [[4, 5, 6, 7], [0, 1, 2, 3]]
-        for k in range(1, 4):
-            tt(A("zt", C * k, C * k + C), A("gt", C * k, C * k + C), A("gt", C * k - 4, C * k + C - 4), ALU.add)
-            if k == 2 or k == 3:
-                h = k - 2
-                quant("z", H * h, H * h + H, A("zt", 4 * H * h, 4 * H * h + 4 * H))
-                for b in range(4):
-                    mm(banks[h][b], "w", 128 * b, "z", H * h, H * h + H)
+        def layer(h):
+            quant("z", H * h, H * h + H, A("zt", 4 * H * h, 4 * H * h + 4 * H))
+            for b in range(4): mm(banks[h][b], "w", 128 * b, "z", H * h, H * h + H)
+        def part(name, h, b): return A(name, 4 * H * h + b, 4 * H * h + 4 * H, 4)
+        def summed(h, b): tt(part("x32", h, b), PS(banks[h][b], H), part("z32", h, b), ALU.add)
+        for lo, hi in GS: act(*gathered(lo, hi), ACT.Copy)
+        for lo, hi in GV: copy(*gathered(lo, hi))
+        for lo, hi in (GV + GS)[:-1]: add(lo, hi)
+        layer(0)
+        add(*GS[-1])
+        for h in range(2):
+            act(A("z32", 4 * H * h, 4 * H * h + 4 * H), A("zt", 4 * H * h, 4 * H * h + 4 * H), ACT.Copy, scale=32.0)
+        summed(0, 0)
+        layer(1)
         for h in range(2):
             for b in range(4):
-                act(A("z32", C * b + H * h, C * b + H * h + H), A("zt", 4 * H * h + b, 4 * H * h + 4 * H, 4), ACT.Copy, scale=32.0)
-        def part(name, h, b): return A(name, C * b + H * h, C * b + H * h + H)
-        def xpart(h, b): return A("xt", 4 * H * h + b, 4 * H * h + 4 * H, 4)
-        for b in range(4):
-            tt(part("x32", 0, b), PS(banks[0][b], H), part("z32", 0, b), ALU.add)
-        for b in range(4):
-            act(xpart(0, b), part("x32", 0, b), ACT.Copy, scale=1.0 / 32)
-        if lastr:
-            act(A("lo"), IND(A("pl"), A("ofl")), ACT.Copy)
-            dma("Y", T.ls[:, 0:C], rows("lo"), [A("lo")], [])
-        for b in range(4):
-            tt(part("x32", 1, b), PS(banks[1][b], H), part("z32", 1, b), ALU.add)
-            if b > 0:
-                ts(xpart(1, b - 1), part("x32", 1, b - 1), 1.0 / 32, ALU.mult)
-        quant_x(0, "v" if lastr else "u1")
-        ts(xpart(1, 3), part("x32", 1, 3), 1.0 / 32, ALU.mult)
-        quant_x(1, "v" if lastr else "u1")
+                if h == 1 and b == 3: scores(0, "v" if lastr else "u1")
+                if h or b: summed(h, b)
+                if h == 0 or b < SD: act(part("xt", h, b), part("x32", h, b), ACT.Copy, scale=1.0 / 32)
+        for b in range(SD, 4): ts(part("xt", 1, b), part("x32", 1, b), 1.0 / 32, ALU.mult)
 
-    for h in range(2):
-        dma("Y", T.oc[:, 4 * H * h:4 * H * h + 4 * H], T.q_x[:, H * h:H * h + H].bitcast(dt.uint8), [A("q_x", H * h, H * h + H)], [])
-        act(A("yy", H * h, H * h + H), PS(4 + 2 * h, H), ACT.Copy)
-        dma("S", T.y[:, H * h:H * h + H], T.yy[:, H * h:H * h + H], [A("yy", H * h, H * h + H)], [])
+    dma("Y", T.oc[:, 0:4 * H], T.q_x[:, 0:H].bitcast(dt.uint8), [A("q_x", 0, H)], [])
+    act(A("yy", 0, H), PS(4, H), ACT.Copy)
+    dma("S", T.y[:, 0:H], T.yy[:, 0:H], [A("yy", 0, H)], [])
+    tt(A("lx"), A("ww", 0, C), A("k16"), ALU.mult)
+    scores(1, "v")
+    dma("Y", T.oc[:, 4 * H:4 * C], T.q_x[:, H:C].bitcast(dt.uint8), [A("q_x", H, C)], [])
+    scan(A("lf"), A("cum"), A("lx"), -SM, ALU.max, ALU.min)
+    copy(A("yy", H, C), PS(6, H))
     for k in range(4):
-        dma("Y", T.osc[4 * k:4 * k + 4, :], T.s_x[32 * k:32 * k + 4, :], [A("s_x")], [])
+        dma("YYSS"[k], T.osc[4 * k:4 * k + 4, :], T.s_x[32 * k:32 * k + 4, :], [A("s_x")], [])
+    dma("S", T.y[:, H:C], T.yy[:, H:C], [A("yy", H, C)], [])
+    hold(A("ly"), A("lf"), A("rs16b"))
+    copy(A("ofl"), A("ly", 15, C, 16))
+    copy(A("lo"), IND(A("pl"), A("ofl")))
+    dma("Y", T.ls[:, 0:C], rows("lo"), [A("lo")], [])
     _emit(g, T, ops)

@@ -15,20 +15,20 @@ F8 = "float8_e4m3fn_x4"
 TILES = [(0, 19, 18, 17), (16, 15, 14, 13), (12, 11, 10, 9), (8, 7, 6, 5), (4, 3, 2, 1)]
 TW = [320, 256, 192, 128, 128]
 TO = [0, 320, 576, 768, 896]
-S_ONLY = (9, 8, 7, 13, 12)
-V_SUM = (4, 3, 2, 1)
+S_ONLY = (9, 8, 7, 12, 11)
+V_SUM = (4, 3, 2, 1, 6, 5)
 NSS = 7
 MW = NS + 2
 B1 = NS + 32
 TB = NS + B1
 GV = [(0, 12), (12, 24)]
 GS = [(24, 40), (40, 60), (60, 80)]
-SD = 2
-POOLS = {"cf": ("float32", (("pf", 4), ("cola", 1), ("colr", 1), ("cl", 1), ("c2", 1), ("j192", NS), ("jg", 128),
+SD = 1
+POOLS = {"cf": ("float32", (("pf", 4), ("co", 1), ("ca", 1), ("c3", 3), ("colr", 1), ("cl", 1), ("c2", 1), ("j192", NS), ("jg", 128),
                             ("m16", H), ("m16n", KEEP), ("rs16", H), ("iod", 16), ("ge", 128))),
          "cb": ("bfloat16", (("sid", NS), ("k4", C), ("k16", C), ("q16", C), ("q4", C), ("eq16", C), ("ramp", 256), ("rsd", C), ("m16h", C),
-                             ("jb", C), ("m4b", C), ("rs4b", C), ("m16b", C), ("rs16b", C), ("rmw", 12 * MW), ("r16", TB))),
-         "af": ("float32", (("f32", NS), ("kk", NS), ("kd", 16), ("acc", 12), ("p2", 12), ("hl", 1), ("lo", C))),
+                             ("jb", C), ("rs4b", C), ("rs16b", C), ("rmw", 12 * MW), ("r16", TB))),
+         "af": ("float32", (("f32", NS), ("kk", NS), ("kd", 16), ("acc", 12), ("p2", 12), ("hl", 1), ("lso", C))),
          "ab": ("bfloat16", (("b1", 2 * B1), ("t1", 2 * TB), ("s1", 2 * TB), ("s16", 24), ("b2", 2 * NS), ("t2", 2 * NS), ("s2", 2 * NS),
                              ("tot", 32), ("fo", NS), ("fw", TB), ("ffp", B1), ("ww", NS + KEEP), ("wm", C),
                              ("lx", C), ("junk2", 12 * NS), ("ms", 16 * MW), ("mss", 12 * MW))),
@@ -42,8 +42,8 @@ def _scratch():
     bf, f32, i32, u16, u8 = "bfloat16", "float32", "int32", "uint16", "uint8"
     for name, n in (("ut", 512), ("vt", 512), ("xt", 1280), ("x32", 1280), ("zt", 1280), ("z32", 1280), ("gt", 1296),
                     ("at", 512), ("vw", 4 * (STAY + KEEP)), ("ct", 4096), ("stmp", 6 * C), ("et", 2048),
-                    ("bt", 512), ("xc", C), ("yc", C), ("rds", C), ("ow", C),
-                    ("xo", C), ("yo", C), ("xk", KEEP), ("yk", KEEP), ("junk", 3200), ("one5", 512)):
+                    ("bt", 512), ("xc", C), ("xd", 128), ("yc", C), ("rds", C), ("ow", C + 32),
+                    ("tw", 2 * C + 32), ("ta", 2 * L + 32), ("junk", 3200), ("one5", 512)):
         sb(name, n, bf)
     for name, n in (("xs", C), ("ys", C), ("ss", C), ("sa", 2 * NS), ("sx", 16), ("rs", 20), ("w2", 20),
                     ("rk", 20), ("kf", KEEP), ("ky", KEEP), ("pl", STAY + KEEP), ("yy", C)):
@@ -58,7 +58,7 @@ def _scratch():
         sb(pool, at, d)
     for name, n in (("pi", 1), ("pj", 4), ("uo32", 12), ("pk", 4)):
         sb(name, n, i32)
-    for name, n in (("uo", 8), ("un", 12), ("u8", 2), ("lp", 2), ("ofr", 20), ("ofa", 24), ("ofs", 56), ("ofk", 14), ("ofb", 32),
+    for name, n in (("uo", 8), ("un", 12), ("u8", 2), ("lp", 2), ("ofr", 20), ("lo", 2), ("la", 2), ("ofa", 16), ("ofk", 32), ("ofb", 32),
                     ("ofp", 12), ("ofg", 80), ("ofl", 20)):
         sb(name, n, u16)
     for name, n in (("u0", 128), ("u1", 128), ("u2", 16), ("ul", 64), ("uf", 256), ("v", 128), ("x", C), ("z", C), ("w", 512),
@@ -85,6 +85,9 @@ def _meets(a, b):
         return False
     if a[3] == b[3] and a[3] > 1 and (a[1] - b[1]) % a[3]:
         return False
+    if min(a[3], b[3]) == 1:
+        s, r = (a, b) if a[3] > 1 else (b, a)
+        return s[1] + max(0, -(-(r[1] - s[1]) // s[3])) * s[3] < min(s[2], r[2])
     return True
 
 
@@ -204,7 +207,6 @@ def rank_program(g, core, T, topo):
     def dma(qn, o, i, rd, wr): op(qn, lambda q: q.dma_start(o, i), rd, wr, kind="d")
     def PS(k, hi, lo=0): return A("ps%d" % k, lo, hi)
     def rows(name): return T.af[0:128:16, PART[name][1]:PART[name][1] + PART[name][2]]
-    def mask(x, src, m): scan(x, src, m, -SM, ALU.max, ALU.min)
     def hold(y, x, reset, low=-SM): scan(y, reset, x, low, ALU.min, ALU.max)
 
     def send(pieces, rd):
@@ -236,16 +238,10 @@ def rank_program(g, core, T, topo):
     iota(A("rsd"), [[-16, 20], [2 * SM, 16]], 128, 0)
     iota(A("jb"), [[1, C]], -128, 0)
     memset(A("one5"), 1.0)
-    memset(A("ow"), 0.0)
-    memset(A("at", 4 * L, 512), 0.0)
-    memset(A("r16"), 1.0 * SM)
-    memset(A("rs4b"), 1.0 * SM)
+    for o in (A("ow"), A("at", 4 * L, 512), A("b1"), A("tw", 0, L), A("tw", C, C + L)):
+        act(o, A("one5", 0, o[1][0][2] - o[1][0][1]), ACT.Copy, scale=0.0)
     for m in range(5):
         memset(A("ct", 4 * TO[m] + 64 * TILES[m][3], 4 * (TO[m] + TW[m])), 0.0)
-    memset(A("b1"), 0.0)
-    memset(A("ffp"), 0.0)
-    memset(A("r16", 0, TB, 16), 0.0)
-    memset(A("rs4b", 0, C, 4), -1.0 * SM)
     ts(A("pj", 0, 1), A("pi"), 15, ALU.bitwise_and)
     ts(A("pj", 1, 2), A("pi"), 3, ALU.bitwise_and)
     ts(A("pj", 2, 3), A("pi"), 2, ALU.logical_shift_right, 3, ALU.bitwise_and)
@@ -255,21 +251,8 @@ def rank_program(g, core, T, topo):
     quant("u0", 0, 128, A("ut"))
     copy(A("pf"), A("pj"))
     pr, p4, pe, pg = [A("pf", k, k + 1) for k in range(4)]
-    memset(A("rs", 0, 1), 0.0)
     ts(A("u8", 0, 1), A("pk", 0, 1), 16.0, ALU.mult)
-    copy(A("un"), A("uo32"))
-    memset(A("ms", NS + 1, 12 * MW, MW), -2.0 * KEEP)
     pick("u1", 0, 128, "u0", 0, 128, A("uo"))
-    mine = senders(rank)
-    other = [[r for r in ((s + 1) % n, (s + 2) % n) if r != rank][0] for s in mine]
-    place = [senders(d).index(s) for d, s in zip(other, mine)]
-    pick("u2", 0, 16, "u0", 0, 128, A("u8", 0, 1))
-    send([(d, T.q_u2[:, 0:16].bitcast(dt.uint8), T.q_ul[:, 32 * a:32 * a + 16].bitcast(dt.uint8), "arru") for d, a in zip(other, place)], [A("q_u2")])
-    send([(d, T.s_u2[:, 0:16], T.s_ul[:, 32 * a:32 * a + 16], "arru") for d, a in zip(other, place)], [A("s_u2")])
-    iota(A("q4"), [[0, 80], [1, 4]], 0, 0)
-    iota(A("j192"), [[1, NS]], 1, 0)
-    iota(A("ramp"), [[16, 16], [0, 16]], 0, 0)
-    for b in range(2): unit_tile(b)
     ts(A("eq16"), A("q16"), pr, ALU.is_equal, 0.5, ALU.subtract)
     act(A("m16"), A("eq16", 0, H), ACT.Copy, scale=2 * BIG)
     act(A("rs16"), A("rs16b", 0, H), ACT.Copy, scale=BIG / SM)
@@ -293,19 +276,33 @@ def rank_program(g, core, T, topo):
         else:
             act(A("junk", 8 * c * (c - 1), 8 * c * (c + 1)), lane(c), ACT.Identity, acc=A("rs", c, c + 1))
     def quant_c(m): quant("c", TO[m], TO[m] + TW[m], A("ct", 4 * TO[m], 4 * (TO[m] + TW[m])))
-    def sum_c(m, start=False, stop=False): mm(2, "b", 0, "c", TO[m], TO[m] + TW[m], start, stop)
+    def sum_c(m): mm(2 + m // 3, "b", 0, "c", TO[m], TO[m] + TW[m], m in (0, 4), m in (2, 3))
     def shared(m): return [c for c in TILES[m] if c and c not in S_ONLY]
     def scores(h, w):
         quant("x", H * h, H * h + H, A("xt", 4 * H * h, 4 * H * h + 4 * H))
         mm(4 + 2 * h, w, 0, "x", H * h, H * h + H)
         if w == "u1": mm(5 + 2 * h, w, 0, "x", H * h, H * h + H)
+    def spread(a): pick("uf", 128 * a, 128 * a + 128, "ul", 32 * a, 32 * a + 16, A("un", 0, 8), arr=[("arru", 4 * half)])
     def quant_e(b): quant("e", 128 * b, 128 * b + 128, A("et", 512 * b, 512 * b + 512))
 
     scores(0, "u1")
+    mine = senders(rank)
+    other = [[r for r in ((s + 1) % n, (s + 2) % n) if r != rank][0] for s in mine]
+    place = [senders(d).index(s) for d, s in zip(other, mine)]
+    pick("u2", 0, 16, "u0", 0, 128, A("u8", 0, 1))
+    send([(d, T.q_u2[:, 0:16].bitcast(dt.uint8), T.q_ul[:, 32 * a:32 * a + 16].bitcast(dt.uint8), "arru") for d, a in zip(other, place)], [A("q_u2")])
+    send([(d, T.s_u2[:, 0:16], T.s_ul[:, 32 * a:32 * a + 16], "arru") for d, a in zip(other, place)], [A("s_u2")])
+    iota(A("q4"), [[0, 80], [1, 4]], 0, 0)
+    iota(A("j192"), [[1, NS]], 1, 0)
+    iota(A("ramp"), [[16, 16], [0, 16]], 0, 0)
+    iota(A("r16"), [[0, TB // 16], [SM, 16]], 0, 0)
+    for b in range(2): unit_tile(b)
+    iota(A("rs4b"), [[0, 80], [2 * SM, 4]], -SM, 0)
+    iota(A("ffp"), [[0, B1]], 0, 0)
     ts(A("ge"), A("jg"), pg, ALU.is_equal)
+    memset(A("rs", 0, 1), 0.0)
     for b in range(4):
         act(A("bt", b, 512, 4), A("ge"), ACT.Copy)
-    memset(A("rmw", MW * NSS), 1.0)
     for t in range(R):
         lastr = t == R - 1
         act(A("ss", 0, H), PS(5, H), ACT.Copy)
@@ -314,13 +311,9 @@ def rank_program(g, core, T, topo):
         act(A("ss", H, C), PS(7, H), ACT.Copy)
         hold(A("ys", 0, H), A("xs", 0, H), A("rs16", 0, H), -BIG)
         if t == 0:
-            memset(A("rmw", 0, 12 * MW, MW), 0.0)
-            ts(A("cola"), p4, 512.0, ALU.add)
+            tt(A("pk", 1, 2), A("pj", 0, 1), A("pj", 3, 4), ALU.add)
+            for k, most in enumerate((15.0, 3.0, 5.0)): ts(A("c3", k, k + 1), pr, most, ALU.min, 16.0, ALU.mult)
             ts(A("colr"), pr, -1.0, ALU.mult, 15.0 + 256, ALU.add)
-            memset(A("vw", 0, 4), 0.0)
-            memset(A("vw", 4 + 4 * NS, 4 * STAY), 0.0)
-            memset(A("pl", 0, 1), 0.0)
-            memset(A("pl", NS + 1, STAY), 0.0)
         tt(A("xs", H, C), PS(6, H), A("m16", 0, H), ALU.min)
         first = [c for c in S_ONLY if 16 * c + 16 <= H]
         for c in first: strip(c)
@@ -332,59 +325,68 @@ def rank_program(g, core, T, topo):
         for c in rest: strip(c)
         for c in rest: strip_sum(c)
         tt(A("ct", 4 * H, 4 * C, 4), A("ys", H, C), PS(6, H), ALU.is_ge)
+        if t == 0: quant("b", 0, 128, A("bt"))
+        done = [4]
         for m in range(4):
-            for k, c in enumerate(shared(m)):
+            for c in shared(m):
                 strip(c)
-                strip_sum(c)
-                if m == 0 and k == 0: quant_c(4)
-                if m == 0 and k == 1 and t == 0: quant("b", 0, 128, A("bt"))
-                if m and k == 0:
-                    quant_c(m - 1)
-                    sum_c(m - 1, start=m == 1)
-                    if m == 1: sum_c(4)
+                if c not in V_SUM: strip_sum(c)
+                if done:
+                    quant_c(done[0])
+                    sum_c(done.pop(0))
+            done.append(m)
         if t == 0:
             ts(A("m16h"), A("eq16"), 2.0 * SM, ALU.mult, -128.0 - SM, ALU.add)
         scan(A("rds"), A("rsd"), A("ct", 0, 4 * C, 4), SM, ALU.min, ALU.add)
-        quant_c(3)
-        sum_c(3, stop=True)
-        for c in shared(4): strip_sum(c)
-        if t == 0:
-            act(A("q4"), A("q4"), ACT.Abs, scale=-1.0, bias=pe)
-            act(A("m16b"), A("eq16"), ACT.Copy, scale=2.0 * SM)
-            act(A("m4b"), A("q4"), ACT.Identity, scale=-2.0 * SM, bias=1.0 * SM)
+        for m in done:
+            quant_c(m)
+            sum_c(m)
         tt(A("xc"), PS(2, C), A("m16h"), ALU.add)
-        tt(A("w2"), A("rds", 15, C, 16), A("rs"), ALU.add)
-        hold(A("yc"), A("xc"), A("rs16b"))
+        for c in V_SUM: strip_sum(c)
         if t == 0:
-            tt(A("pk", 1, 2), A("pj", 0, 1), A("pj", 3, 4), ALU.add)
+            for b in range(4): act(A("x32", C * b, C * b + C), A("xt", b, 4 * C, 4), ACT.Copy, scale=32.0)
+            ts(A("pk", 2, 3), A("pk", 1, 2), 1, ALU.bitwise_and)
+        tt(A("xd"), PS(3, 128), A("xc", 0, 128), ALU.add)
+        hold(A("yc", 128), A("xc", 128), A("rs16b", 128))
+        tt(A("w2"), A("rds", 15, C, 16), A("rs"), ALU.add)
+        if t == 0:
             for k in range(R): memset(A("km%d" % k, 14, 15), -BIG)
+        hold(A("yc", 0, 128), A("xd"), A("rs16b", 0, 128))
+        if t == 0:
+            ts(A("co"), A("pk", 2, 3), C + 16.0, ALU.mult, 15.0, ALU.add)
+            ts(A("ca"), A("pk", 2, 3), L + 16.0, ALU.mult, 15.0, ALU.add)
         tt(A("rk"), A("yc", 15, C, 16), A("w2"), ALU.subtract)
-        if t == 0: quant_e(0)
+        if t == 0:
+            ts(A("lo", 0, 1), A("c3", 0, 1), A("co"), ALU.add)
+            ts(A("la", 0, 1), A("c3", 2, 3), A("ca"), ALU.add)
+            ts(A("lo", 1, 2), A("c3", 1, 2), A("co"), ALU.add, 256.0, ALU.add)
         ts(A("ofr"), A("rk"), A("colr"), ALU.add)
-        if t == 0: ts(A("pk", 2, 3), A("pk", 1, 2), 1, ALU.bitwise_and)
-        scatter(A("ow"), A("ofr"), A("jb"))
-        mask(A("xo", 0, L), A("ow", 0, L), A("m4b", 0, L))
-        mask(A("xk"), A("ow", L, C), A("m16b", 0, KEEP))
-        hold(A("yo", 0, L), A("xo", 0, L), A("rs4b", 0, L))
-        mask(A("xo", L, C), A("ow", L, C), A("m4b", 0, KEEP))
-        ts(A("ofa"), A("yo", 3, L, 4), 4.0, ALU.mult, A("cola"), ALU.add)
-        hold(A("yk"), A("xk"), A("rs16b", 0, KEEP))
-        act(A("at", 192, 384), IND(A("xt"), A("ofa", 12, 24)), ACT.Copy)
-        copy(A("at", 0, 192), IND(A("xt"), A("ofa", 0, 12)))
-        hold(A("yo", L, C), A("xo", L, C), A("rs4b", 0, KEEP))
-        ts(A("ofk"), A("yk", 15, KEEP, 16), 128.0, ALU.add)
+        if t == 0:
+            quant_e(0)
+            copy(A("un"), A("uo32"))
+        scatter(A("ow", 16, 16 + C), A("ofr"), A("jb"))
+        turn(A("ta", 0, L), A("ow", 16, 16 + L))
+        turn(A("ta", L), A("ow", 0, L + 32))
+        turn(A("tw", L, C), A("ow", 16 + L, 16 + C))
+        ts(A("ofa"), IND(A("ta"), A("la", 0, 1)), 128.0, ALU.add)
+        turn(A("tw", C + L), A("ow", L))
+        def row_of(b, off): return IND(A("x32", C * b, C * b + C), off)
+        for b in range(2):
+            act(A("at", 2 + b, 4 * L, 4), row_of(2 + b, A("ofa", 0, L // 16)), ACT.Copy, scale=1.0 / 32)
+            ts(A("at", b, 4 * L, 4), row_of(b, A("ofa", 0, L // 16)), 1.0 / 32, ALU.mult)
+        ts(A("ofk"), IND(A("tw"), A("lo")), 128.0, ALU.add)
+        stay = A("ofk", L // 16, C // 16)
         an, ln, km, kin = "a%d" % t, "l%d" % t, "km%d" % t, "kin%d" % t
         quant(an, 0, 128, A("at"))
         to = [(rank + 1) % n, (rank + 2) % n]
         at = [L * senders(d).index(rank) for d in to]
         send([(d, T["q_" + an][:, 0:L].bitcast(dt.uint8), T["q_" + ln][:, a:a + L].bitcast(dt.uint8), "arra%d" % t) for d, a in zip(to, at)], [A("q_" + an)])
         send([(d, T["s_" + an][:, 0:L], T["s_" + ln][:, a:a + L], "arra%d" % t) for d, a in zip(to, at)], [A("s_" + an)])
-        ts(A("ofs"), A("yo", L + 3, C, 4), 4.0, ALU.mult, A("cola"), ALU.add)
-        copy(A("kf"), IND(A("ss"), A("ofk")))
+        copy(A("kf"), IND(A("ss"), stay))
         if t == 0:
             act(A("m16n"), A("eq16", 0, KEEP), ACT.Copy, scale=-2 * BIG)
-            quant_e(1)
-        act(A("vw", 4 * STAY, 4 * (STAY + KEEP)), IND(A("xt"), A("ofs")), ACT.Copy, scale=0.5)
+        for b in range(4): act(A("vw", 4 * STAY + b, 4 * (STAY + KEEP), 4), row_of(b, stay), ACT.Copy, scale=1.0 / 64)
+        if t == 0: spread(0)
         tt(A("sx", 0, 14), A("kf", 15, KEEP, 16), A("m16", 0, 14), ALU.min)
         scan(A("ky"), A("m16n"), A("kf"), -BIG, ALU.min, ALU.max)
         reduce(A(km, 15, 16), A("sx", 0, 14), ALU.max)
@@ -393,16 +395,17 @@ def rank_program(g, core, T, topo):
         memset(A("ww"), 1.0)
         if t == 0:
             for b in range(2, 4): unit_tile(b)
-            for a in range(2): pick("uf", 128 * a, 128 * a + 128, "ul", 32 * a, 32 * a + 16, A("un", 0, 8), arr=[("arru", 4 * half)])
+            iota(A("rmw", MW * NSS), [[0, 12 - NSS], [SM, MW]], -2 * KEEP, 0)
+            spread(1)
+            memset(A("ms", NS + 1, 12 * MW, MW), 0.0)
+            quant_e(1)
             ts(A("cl"), A("pk", 2, 3), NS + 16.0, ALU.mult, 15.0, ALU.add)
             ts(A("c2"), pr, 11.0, ALU.min, 16.0, ALU.mult)
-            ts(A("lev1", 0, NS), A("q16", 0, NS), pr, ALU.is_gt, 1.0 / 16, ALU.mult)
-            ts(A("lev1", NS), A("ramp", 0, NS), 1.0 / 256, ALU.mult, -KEEP / 2, ALU.add)
             ts(A("lp", 0, 1), A("c2"), A("cl"), ALU.add)
-            tt(A("lev"), A("lev1", 0, NS), A("lev1", NS), ALU.add)
-            ts(A("iod"), A("ramp", 0, 256, 16), 1.0 / 256, ALU.mult, 1.0 / 32 - KEEP / 2, ALU.add)
         if t == 1:
             quant("v", 0, 128, A("vt"))
+            memset(A("pl", 0, 1), 0.0)
+            memset(A("pl", NS + 1, STAY), 0.0)
         copy(A("gt", 0, 4), A("vw", 4 * STAY, 4 * STAY + 4))
         def unpack(b):
             mm(4 + b, "e", 128 * b, ln, 0, NS)
@@ -428,8 +431,8 @@ def rank_program(g, core, T, topo):
             for s, lo, hi, w, a in views[e]:
                 tt(A("b2", NS * e + lo, NS * e + hi), IND(A(w, a, a + 16), A("ofb", 16 * e + lo // 16, 16 * e + hi // 16)),
                    A("sa", NS * e + lo, NS * e + hi), ALU.is_gt)
-        def turn2(e): turn(A("t2", NS * e, NS * e + NS), A("b2", NS * e, NS * e + NS))
-        def sum2(e): scan(A("s2", NS * e, NS * e + NS), A("r16", 0, NS), A("t2", NS * e, NS * e + NS), 0.0, ALU.min, ALU.add)
+        def turn2(e, lo, hi): turn(A("t2", NS * e + lo, NS * e + hi), A("b2", NS * e + lo, NS * e + hi))
+        def sum2(e, lo, hi): scan(A("s2", NS * e + lo, NS * e + hi), A("r16", lo, hi), A("t2", NS * e + lo, NS * e + hi), 0.0, ALU.min, ALU.add)
         def total(e): tt(A("tot", 16 * e, 16 * e + 12), A("s2", NS * e + 15, NS * e + NS, 16), A("s16", 12 * e, 12 * e + 12), ALU.add)
         steps = [runs, turns, sums, lists, places]
         runs(0)
@@ -439,29 +442,41 @@ def rank_program(g, core, T, topo):
             if k == 1:
                 for b in range(4 if t else 2): unpack(b)
         if t == 0:
-            act(A("k4"), A("m4b"), ACT.Relu, scale=1 / (TINY * SM))
+            act(A("q4"), A("q4"), ACT.Abs, scale=-1.0, bias=pe)
+            act(A("k4"), A("q4"), ACT.Relu, scale=-1 / TINY, bias=1 / TINY)
             act(A("sid"), A("j192"), ACT.Copy, scale=TINY)
             for b in range(2, 4):
                 quant_e(b)
                 unpack(b)
         if t == 1:
-            act(A("k16"), A("m16b"), ACT.Relu, scale=1 / (TINY * SM))
+            act(A("k16"), A("eq16"), ACT.Relu, scale=2 / TINY)
             act(A("pl", 1, NS + 1), A("j192"), ACT.Identity, bias=C - 1.0)
         if lastr:
-            act(A("pl", STAY, STAY + KEEP), A("ow", L, C), ACT.Identity, bias=128.0)
-        turn2(0)
+            act(A("pl", STAY, STAY + KEEP), A("ow", 16 + L, 16 + C), ACT.Identity, bias=128.0)
+        turn2(0, 0, NS)
         places(1)
-        sum2(0)
-        turn2(1)
+        sum2(0, 0, NS)
+        for lo in (0, L): turn2(1, lo, lo + L)
         total(0)
-        sum2(1)
-        copy(A("fo"), IND(A("tot", 0, 12), A("un")))
+        for lo in (0, L): sum2(1, lo, lo + L)
+        def spread_tot(e, lo): return IND(A("tot", 16 * e, 16 * e + 12), A("un", lo // 16, (lo + L) // 16))
+        copy(A("fo", 0, L), spread_tot(0, 0))
         total(1)
-        tt(A("fw", 0, NS), IND(A("tot", 16, 28), A("un")), A("fo"), ALU.max)
+        copy(A("fo", L, NS), spread_tot(0, L))
+        if t == 0:
+            ts(A("lev1", 0, NS), A("q16", 0, NS), pr, ALU.is_gt, 1.0 / 16, ALU.mult)
+        for lo in (0, L): tt(A("fw", lo, lo + L), spread_tot(1, lo), A("fo", lo, lo + L), ALU.max)
+        if t == 0: ts(A("lev1", NS), A("ramp", 0, NS), 1.0 / 256, ALU.mult, -KEEP / 2, ALU.add)
         ff = A("ffp", 16, 16 + NS)
-        turn(ff, A("fw", 0, NS))
+        def keys(lo): tt(A("kk", lo, lo + L), A("ffp", 16 + lo, 16 + lo + L), A("lev", lo, lo + L), ALU.add)
+        turn(A("ffp", 16, 16 + L), A("fw", 0, L))
+        if t == 0: ts(A("iod"), A("ramp", 0, 256, 16), 1.0 / 256, ALU.mult, 1.0 / 32 - KEEP / 2, ALU.add)
+        turn(A("ffp", 16 + L, 16 + NS), A("fw", L, NS))
+        if t == 0: tt(A("lev"), A("lev1", 0, NS), A("lev1", NS), ALU.add)
+        else: keys(0)
         turn(A("fw", NS, TB), A("ffp"))
-        tt(A("kk"), ff, A("lev"), ALU.add)
+        if t == 0: keys(0)
+        keys(L)
         fd = IND(A("fw"), A("lp", 0, 1))
         tt(A("kd"), fd, A("iod"), ALU.add)
         def key(c): return A("kd", c, c + 1)
@@ -474,7 +489,7 @@ def rank_program(g, core, T, topo):
         for c in range(NSS, 12):
             ts(A("ms", MW * c, MW * c + NS), A("kk"), key(c), ALU.is_lt, 2.0, ALU.mult)
         for lo, hi in ((NSS, 10), (10, 12)):
-            scan(A("mss", MW * lo, MW * hi), A("rmw", MW * lo, MW * hi), A("ms", MW * lo, MW * hi), 0.0, ALU.mult, ALU.add)
+            scan(A("mss", MW * lo, MW * hi), A("rmw", MW * lo, MW * hi), A("ms", MW * lo, MW * hi), 0.0, ALU.min, ALU.add)
         e = NSS - 1
         ts(A("hl"), A("ms", MW * e + NS, MW * e + NS + 1), 0.5, ALU.mult, NS / 2, ALU.add)
         tt(A("p2", 0, e), A("acc", 0, e), A("ms", NS, MW * e, MW), ALU.add)
@@ -483,10 +498,14 @@ def rank_program(g, core, T, topo):
         ts(A("ofp", e, NSS), A("acc", e, NSS), 0.5, ALU.mult, A("hl"), ALU.add)
         scatter(A("ww"), A("ofp"), A("sid"))
         scan(A("cum"), A("one5", 0, C), A("ww", 0, C), STAY - 1, ALU.mult, ALU.add)
-        tt(A("wm"), A("ww", 0, C), A("k4"), ALU.mult)
-        scan(A("wx"), A("cum"), A("wm"), -SM, ALU.max, ALU.min)
-        hold(A("wy"), A("wx"), A("rs4b"))
-        ts(A("ofg"), A("wy", 3, C, 4), 4.0, ALU.mult, p4, ALU.add)
+        halves = ((0, H), (H, C))
+        for lo, hi in halves: tt(A("wm", lo, hi), A("ww", lo, hi), A("k4", lo, hi), ALU.mult)
+        for lo, hi in halves: scan(A("wx", lo, hi), A("cum", lo, hi), A("wm", lo, hi), -SM, ALU.max, ALU.min)
+        if t == 0: memset(A("vw", 0, 4), 0.0)
+        for lo, hi in halves: hold(A("wy", lo, hi), A("wx", lo, hi), A("rs4b", lo, hi))
+        if t == 0: memset(A("vw", 4 + 4 * NS, 4 * STAY), 0.0)
+        for lo, hi in halves: ts(A("ofg", lo // 4, hi // 4), A("wy", lo + 3, hi, 4), 4.0, ALU.mult, p4, ALU.add)
+        if lastr: tt(A("lx", 0, H), A("ww", 0, H), A("k16", 0, H), ALU.mult)
         def gathered(lo, hi): return A("gt", 16 * lo + 4, 16 * hi + 4), IND(A("vw"), A("ofg", lo, hi))
         def add(lo, hi): tt(A("zt", 16 * lo, 16 * hi), A("gt", 16 * lo + 4, 16 * hi + 4), A("gt", 16 * lo, 16 * hi), ALU.add)
         banks = [[4, 5, 6, 7], [0, 1, 2, 3]]
@@ -494,12 +513,14 @@ def rank_program(g, core, T, topo):
             quant("z", H * h, H * h + H, A("zt", 4 * H * h, 4 * H * h + 4 * H))
             for b in range(4): mm(banks[h][b], "w", 128 * b, "z", H * h, H * h + H)
         def part(name, h, b): return A(name, 4 * H * h + b, 4 * H * h + 4 * H, 4)
-        def summed(h, b): tt(part("x32", h, b), PS(banks[h][b], H), part("z32", h, b), ALU.add)
+        def row(h, b): return A("x32", C * b + H * h, C * b + H * h + H)
+        def summed(h, b): tt(row(h, b), PS(banks[h][b], H), part("z32", h, b), ALU.add)
         for lo, hi in GS: act(*gathered(lo, hi), ACT.Copy)
         for lo, hi in GV: copy(*gathered(lo, hi))
         for lo, hi in (GV + GS)[:-1]: add(lo, hi)
         layer(0)
         add(*GS[-1])
+        if lastr: tt(A("lx", H, C), A("ww", H, C), A("k16", H, C), ALU.mult)
         for h in range(2):
             act(A("z32", 4 * H * h, 4 * H * h + 4 * H), A("zt", 4 * H * h, 4 * H * h + 4 * H), ACT.Copy, scale=32.0)
         summed(0, 0)
@@ -508,22 +529,22 @@ def rank_program(g, core, T, topo):
             for b in range(4):
                 if h == 1 and b == 3: scores(0, "v" if lastr else "u1")
                 if h or b: summed(h, b)
-                if h == 0 or b < SD: act(part("xt", h, b), part("x32", h, b), ACT.Copy, scale=1.0 / 32)
-        for b in range(SD, 4): ts(part("xt", 1, b), part("x32", 1, b), 1.0 / 32, ALU.mult)
+                if h == 0 or b < SD: act(part("xt", h, b), row(h, b), ACT.Copy, scale=1.0 / 32)
+        for b in range(SD, 3): ts(part("xt", 1, b), row(1, b), 1.0 / 32, ALU.mult)
+        if lastr: scan(A("lf"), A("cum"), A("lx"), -SM, ALU.max, ALU.min)
+        ts(part("xt", 1, 3), row(1, 3), 1.0 / 32, ALU.mult)
 
     dma("Y", T.oc[:, 0:4 * H], T.q_x[:, 0:H].bitcast(dt.uint8), [A("q_x", 0, H)], [])
     act(A("yy", 0, H), PS(4, H), ACT.Copy)
     dma("S", T.y[:, 0:H], T.yy[:, 0:H], [A("yy", 0, H)], [])
-    tt(A("lx"), A("ww", 0, C), A("k16"), ALU.mult)
+    hold(A("ly"), A("lf"), A("rs16b"))
     scores(1, "v")
     dma("Y", T.oc[:, 4 * H:4 * C], T.q_x[:, H:C].bitcast(dt.uint8), [A("q_x", H, C)], [])
-    scan(A("lf"), A("cum"), A("lx"), -SM, ALU.max, ALU.min)
+    copy(A("ofl"), A("ly", 15, C, 16))
+    act(A("lso"), IND(A("pl"), A("ofl")), ACT.Copy)
     copy(A("yy", H, C), PS(6, H))
     for k in range(4):
-        dma("YYSS"[k], T.osc[4 * k:4 * k + 4, :], T.s_x[32 * k:32 * k + 4, :], [A("s_x")], [])
-    dma("S", T.y[:, H:C], T.yy[:, H:C], [A("yy", H, C)], [])
-    hold(A("ly"), A("lf"), A("rs16b"))
-    copy(A("ofl"), A("ly", 15, C, 16))
-    copy(A("lo"), IND(A("pl"), A("ofl")))
-    dma("Y", T.ls[:, 0:C], rows("lo"), [A("lo")], [])
+        dma("Y", T.osc[4 * k:4 * k + 4, :], T.s_x[32 * k:32 * k + 4, :], [A("s_x")], [])
+    dma("Y", T.y[:, H:C], T.yy[:, H:C], [A("yy", H, C)], [])
+    dma("S", T.ls[:, 0:C], rows("lso"), [A("lso")], [])
     _emit(g, T, ops)

from concourse.bass import DstId, RemoteDMATransfer
from concourse.mybir import dt, AluOpType, ActivationFunctionType, AxisListType

ALU, ACT = AluOpType, ActivationFunctionType

C, L, R = 320, 96, 3
KEEP = C - L
NS = 2 * L
H = C // 2
BIG = 1.0e25
SM = 2048
STAY = 200
TINY = 2.0 ** -19
F8 = "float8_e4m3fn_x4"
TILES = [(0, 19, 18, 17), (16, 15, 14, 13), (12, 11, 10, 9), (8, 7, 6, 5), (4, 3, 2, 1)]
TW = [320, 256, 192, 128, 128]
TO = [0, 320, 576, 768, 896]
S_ONLY = (9, 8, 7, 12, 11)
V_SUM = (4, 3, 2, 1, 6, 5)
NSS = 7
MW = NS + 2
B1 = NS + 32
TB = NS + B1
GV = [(0, 12), (12, 24)]
GS = [(24, 40), (40, 60), (60, 80)]
SD = 1
POOLS = {"cf": ("float32", (("pf", 4), ("co", 1), ("ca", 1), ("c3", 3), ("colr", 1), ("cl", 1), ("c2", 1), ("j192", NS), ("jg", 128),
                            ("m16", H), ("m16n", KEEP), ("rs16", H), ("iod", 16), ("ge", 128))),
         "cb": ("bfloat16", (("sid", NS), ("k4", C), ("k16", C), ("q16", C), ("q4", C), ("eq16", C), ("ramp", 256), ("rsd", C), ("m16h", C),
                             ("jb", C), ("rs4b", C), ("rs16b", C), ("rmw", 12 * MW), ("r16", TB))),
         "af": ("float32", (("f32", NS), ("kk", NS), ("kd", 16), ("acc", 12), ("p2", 12), ("hl", 1), ("lso", C))),
         "ab": ("bfloat16", (("b1", 2 * B1), ("t1", 2 * TB), ("s1", 2 * TB), ("s16", 24), ("b2", 2 * NS), ("t2", 2 * NS), ("s2", 2 * NS),
                             ("tot", 32), ("fo", NS), ("fw", TB), ("ffp", B1), ("ww", NS + KEEP), ("wm", C),
                             ("lx", C), ("junk2", 12 * NS), ("ms", 16 * MW), ("mss", 12 * MW))),
         "ah": ("float16", (("cum", C), ("wx", C), ("wy", C), ("lf", C), ("ly", C)))}
PART = {}


def _scratch():
    s = {}
    def sb(name, n, d): s[name] = ("sbuf", [128, n], d)
    bf, f32, i32, u16, u8 = "bfloat16", "float32", "int32", "uint16", "uint8"
    for name, n in (("ut", 512), ("vt", 512), ("xt", 1280), ("x32", 1280), ("zt", 1280), ("z32", 1280), ("gt", 1296),
                    ("at", 512), ("vw", 4 * (STAY + KEEP)), ("ct", 4096), ("stmp", 6 * C), ("et", 2048),
                    ("bt", 512), ("xc", C), ("xd", 128), ("yc", C), ("rds", C), ("ow", C + 32),
                    ("tw", 2 * C + 32), ("ta", 2 * L + 32), ("junk", 3200), ("one5", 512)):
        sb(name, n, bf)
    for name, n in (("xs", C), ("ys", C), ("ss", C), ("sa", 2 * NS), ("sx", 16), ("rs", 20), ("w2", 20),
                    ("rk", 20), ("kf", KEEP), ("ky", KEEP), ("pl", STAY + KEEP), ("yy", C)):
        sb(name, n, f32)
    for name, n in (("lev", NS), ("lev1", 2 * NS)):
        sb(name, n, "float16")
    for pool, (d, parts) in POOLS.items():
        at = 0
        for name, n in parts:
            PART[name] = (pool, at, n)
            at += -(-n // 16) * 16
        sb(pool, at, d)
    for name, n in (("pi", 1), ("pj", 4), ("uo32", 12), ("pk", 4)):
        sb(name, n, i32)
    for name, n in (("uo", 8), ("un", 12), ("u8", 2), ("lp", 2), ("ofr", 20), ("lo", 2), ("la", 2), ("ofa", 16), ("ofk", 32), ("ofb", 32),
                    ("ofp", 12), ("ofg", 80), ("ofl", 20)):
        sb(name, n, u16)
    for name, n in (("u0", 128), ("u1", 128), ("u2", 16), ("ul", 64), ("uf", 256), ("v", 128), ("x", C), ("z", C), ("w", 512),
                    ("c", 1024), ("e", 512), ("b", 128)):
        sb("q_" + name, n, F8)
        sb("s_" + name, n, u8)
    for t in range(R):
        sb("q_a%d" % t, 128, F8); sb("s_a%d" % t, 128, u8)
        sb("q_l%d" % t, NS, F8); sb("s_l%d" % t, NS, u8)
        sb("km%d" % t, 16, f32); sb("kin%d" % t, 32, f32)
    for k in range(8):
        s["ps%d" % k] = ("psum", [128, 512], f32)
    return s


SCRATCH = _scratch()
NCS, NDS = 110, 24
SEMAPHORES = (["c%d" % k for k in range(NCS)] + ["d%d" % k for k in range(NDS)] + ["loc", "arru"]
              + ["arra%d" % t for t in range(R)] + ["arrp%d" % t for t in range(R)])


def _meets(a, b):
    if a[0] != b[0] or a[2] <= b[1] or b[2] <= a[1]:
        return False
    if a[3] == b[3] and a[3] > 1 and (a[1] - b[1]) % a[3]:
        return False
    if min(a[3], b[3]) == 1:
        s, r = (a, b) if a[3] > 1 else (b, a)
        return s[1] + max(0, -(-(r[1] - s[1]) // s[3])) * s[3] < min(s[2], r[2])
    return True


def _emit(g, T, ops):
    queue = {"V": g.vector, "S": g.scalar, "T": g.tensor, "G": g, "Y": g.sync}
    known = {q: 0 for q in queue}
    issued = {q: 0 for q in queue}
    wanted = set()
    for i, o in enumerate(ops):
        deps = []
        for j in range(i - 1, -1, -1):
            p = ops[j]
            if p["kind"] == "r" or known[o["q"]] >> j & 1:
                continue
            if p["q"] == "T" and o["q"] == "T":
                continue
            hit = any(_meets(a, b) for a in o["rd"] + o["wr"] for b in p["wr"]) or any(_meets(a, b) for a in o["wr"] for b in p["rd"])
            if not hit and p["q"] != o["q"]:
                hit = any(a[0] == b[0] and a[0].startswith("ps") for a in o["rd"] + o["wr"] for b in p["rd"] + p["wr"])
            if hit:
                deps.append(j)
                known[o["q"]] |= p["known"] | (1 << j) | p["before"]
        o["before"] = issued[o["q"]] if o["kind"] == "c" else 0
        if o["kind"] == "c":
            issued[o["q"]] |= 1 << i
        o["deps"] = deps
        o["known"] = known[o["q"]]
        wanted.update(deps)
    last, count, nd = {}, {}, [0]
    tail = []
    loc = 0
    for i, o in enumerate(ops):
        q = queue[o["q"]]
        for j in o["deps"]:
            q.wait_ge(T.sem[ops[j]["sem"]], ops[j]["val"])
        for name, val in o["arr"]:
            q.wait_ge(T.sem[name], val)
        ins = o["fn"](q)
        if o["kind"] == "r":
            loc += o["loc"]
        elif o["kind"] == "d":
            name = "d%d" % nd[0]
            nd[0] += 1
            o["sem"], o["val"] = name, 16
            ins.then_inc(T.sem[name], 16)
            if i not in wanted:
                tail.append(o)
        elif i in wanted:
            free = [k for k in range(NCS) if k not in last or o["known"] >> last[k] & 1]
            k = min(free, key=lambda k: last.get(k, -1))
            last[k] = i
            count[k] = count.get(k, 0) + 1
            o["sem"], o["val"] = "c%d" % k, count[k]
            ins.then_inc(T.sem["c%d" % k], 1)
    for o in tail:
        queue[o["q"]].wait_ge(T.sem[o["sem"]], o["val"])
    g.wait_ge(T.sem.loc, loc)


def rank_program(g, core, T, topo):
    rank = T.rank_of(core)
    if rank is None:
        return
    n = len(T.cores)
    ops = []

    def senders(r): return sorted([(r - 1) % n, (r - 2) % n])

    def A(name, lo=0, hi=None, step=1):
        if name in PART:
            pool, at, w = PART[name]
            name, lo, hi = pool, at + lo, at + (w if hi is None else hi)
        if hi is None: hi = T[name].shape[1]
        return (T[name][:, lo:hi] if step == 1 else T[name][:, lo:hi:step], [(name, lo, hi, step)])

    def IND(win, off):
        return (win[0].indirect(off[0]), win[1] + off[1])

    def op(q, fn, rd, wr, kind="c", arr=(), loc=0):
        ops.append({"q": q, "fn": fn, "rd": [t for a in rd for t in a[1]], "wr": [t for a in wr for t in a[1]], "kind": kind, "arr": list(arr), "loc": loc})

    def val(s): return s[0] if isinstance(s, tuple) else s
    def aps(*s): return [a for a in s if isinstance(a, tuple)]

    def memset(o, c): op("V", lambda q: q.memset(o[0], c), [], [o])
    def copy(o, i): op("V", lambda q: q.tensor_copy(o[0], i[0]), [i], [o])
    def scatter(win, off, i): op("V", lambda q: q.tensor_copy(win[0].indirect(off[0]), i[0]), [i, off], [win])
    def tt(o, a, b, f): op("V", lambda q: q.tensor_tensor(o[0], a[0], b[0], f), [a, b], [o])
    def ts(o, a, s1, f1, s2=None, f2=None, arr=()):
        if f2 is None: op("V", lambda q: q.tensor_scalar(o[0], a[0], val(s1), None, f1), [a] + aps(s1), [o], arr=arr)
        else: op("V", lambda q: q.tensor_scalar(o[0], a[0], val(s1), val(s2), f1, f2), [a] + aps(s1, s2), [o], arr=arr)
    def scan(o, a, b, init, f0, f1): op("V", lambda q: q.tensor_tensor_scan(o[0], a[0], b[0], float(init), f0, f1), [a, b], [o])
    def reduce(o, i, f): op("V", lambda q: q.tensor_reduce(o[0], i[0], AxisListType.X, f), [i], [o])
    def turn(o, i): op("V", lambda q: q.transpose(o[0], i[0]), [i], [o])
    def pick(to, lo, hi, frm, a, b, off, arr=()):
        o, w = A("q_" + to, lo, hi), A("q_" + frm, a, b)
        op("V", lambda q: q.tensor_copy(o[0].bitcast(dt.uint32), w[0].bitcast(dt.uint32).indirect(off[0])), [w, off], [o], arr=arr)
        copy(A("s_" + to, lo, hi), IND(A("s_" + frm, a, b), off))
    def quant(name, lo, hi, i):
        c, s = A("q_" + name, lo, hi), A("s_" + name, lo, hi)
        op("V", lambda q: q.quantize_mx(c[0], s[0], i[0]), [i], [c, s])
    def act(o, i, f, scale=1.0, bias=None, acc=None):
        kw = {"scale": scale}
        if bias is not None: kw["bias"] = val(bias)
        if acc is not None: kw["accum_out"] = acc[0]
        op("S", lambda q: q.activation(o[0], i[0], f, **kw), [i] + aps(bias), [o] + aps(acc))
    def mm(bank, w, wlo, x, xlo, xhi, start=True, stop=True, arr=()):
        o = A("ps%d" % bank, 0, xhi - xlo)
        a, b, c, d = A("q_" + w, wlo, wlo + 128), A("s_" + w, wlo, wlo + 128), A("q_" + x, xlo, xhi), A("s_" + x, xlo, xhi)
        op("T", lambda q: q.matmul_mx(o[0], a[0], b[0], c[0], d[0], start, stop), [a, b, c, d], [o], arr=arr)
    def iota(o, pat, base, cm, small=True):
        if small: op("G", lambda q: q.iota(o[0], pat, base, cm, allow_small_or_imprecise_dtypes=True), [], [o])
        else: op("G", lambda q: q.iota(o[0], pat, base, cm), [], [o])
    def unit_tile(b):
        def call(q): return q.affine_select(T.et[:, 512 * b:512 * b + 512], T.one5[:], [[1, 512]], ALU.is_equal, 0.0, -b, -4)
        op("G", call, [A("one5")], [A("et", 512 * b, 512 * b + 512)])
    def dma(qn, o, i, rd, wr): op(qn, lambda q: q.dma_start(o, i), rd, wr, kind="d")
    def PS(k, hi, lo=0): return A("ps%d" % k, lo, hi)
    def rows(name): return T.af[0:128:16, PART[name][1]:PART[name][1] + PART[name][2]]
    def hold(y, x, reset, low=-SM): scan(y, reset, x, low, ALU.min, ALU.max)

    def send(pieces, rd):
        trs, tot = [], 0
        for k, (d, src, dst, sem) in enumerate(pieces):
            dc = T.cores[d]
            eng = topo.engines(core, dc)
            h = len(eng) // len(pieces)
            m = sum(1 << e for e in eng[k * h:(k + 1) * h])
            rid, pid, _ = topo.addr(dc)
            trs.append(RemoteDMATransfer(dst_ids=[DstId(rid=rid, pnc=pid)], dma_engine_mask=m, remote_sem=T.sem[sem], src=src, dst=dst))
            tot += h
        op("G", lambda q: q.remote_dma_fused(trs, local_sem=T.sem.loc), rd, [], kind="r", loc=tot)

    half = len(topo.engines(T.cores[senders(rank)[0]], core)) // 2

    dma("S", T.ut[:], T.u[:], [], [A("ut")])
    for h in range(2):
        dma("Y", T.xt[:, 4 * H * h:4 * H * h + 4 * H], T.x[:, 4 * H * h:4 * H * h + 4 * H], [], [A("xt", 4 * H * h, 4 * H * h + 4 * H)])
    dma("Y", T.q_w[:].bitcast(dt.uint8), T.wc[:], [A("xt")], [A("q_w")])
    dma("Y", T.s_w[:], T.ws[:], [], [A("s_w")])
    dma("Y", T.vt[:], T.v[:], [], [A("vt")])

    iota(A("pi"), [[0, 1]], 0, 1, False)
    iota(A("uo32"), [[1, 12]], 0, 0, False)
    iota(A("q16"), [[0, 20], [1, 16]], 0, 0)
    iota(A("rs16b"), [[0, 20], [2 * SM, 16]], -SM, 0)
    iota(A("jg"), [[1, 8], [0, 16]], 0, 0)
    iota(A("rsd"), [[-16, 20], [2 * SM, 16]], 128, 0)
    iota(A("jb"), [[1, C]], -128, 0)
    memset(A("one5"), 1.0)
    for o in (A("ow"), A("at", 4 * L, 512), A("b1"), A("tw", 0, L), A("tw", C, C + L)):
        act(o, A("one5", 0, o[1][0][2] - o[1][0][1]), ACT.Copy, scale=0.0)
    for m in range(5):
        memset(A("ct", 4 * TO[m] + 64 * TILES[m][3], 4 * (TO[m] + TW[m])), 0.0)
    ts(A("pj", 0, 1), A("pi"), 15, ALU.bitwise_and)
    ts(A("pj", 1, 2), A("pi"), 3, ALU.bitwise_and)
    ts(A("pj", 2, 3), A("pi"), 2, ALU.logical_shift_right, 3, ALU.bitwise_and)
    ts(A("pj", 3, 4), A("pi"), 4, ALU.logical_shift_right)
    ts(A("pk", 0, 1), A("pi"), 7, ALU.bitwise_and)
    ts(A("uo"), A("uo32", 0, 8), 16.0, ALU.mult)
    quant("u0", 0, 128, A("ut"))
    copy(A("pf"), A("pj"))
    pr, p4, pe, pg = [A("pf", k, k + 1) for k in range(4)]
    ts(A("u8", 0, 1), A("pk", 0, 1), 16.0, ALU.mult)
    pick("u1", 0, 128, "u0", 0, 128, A("uo"))
    ts(A("eq16"), A("q16"), pr, ALU.is_equal, 0.5, ALU.subtract)
    act(A("m16"), A("eq16", 0, H), ACT.Copy, scale=2 * BIG)
    act(A("rs16"), A("rs16b", 0, H), ACT.Copy, scale=BIG / SM)

    def col(c): return A("ys", 16 * c + 15, 16 * c + 16)
    def lane(c):
        m = [k for k in range(5) if c in TILES[k]][0]
        return A("ct", 4 * TO[m] + TILES[m].index(c), 4 * TO[m] + 64 * c, 4)
    def strip(c):
        if c in S_ONLY:
            k = C * S_ONLY.index(c)
            act(A("stmp", k, k + 16 * c), A("ss", 0, 16 * c), ACT.Sign, scale=-1.0, bias=col(c))
        else:
            ts(lane(c), A("ss", 0, 16 * c), col(c), ALU.is_lt)
    def strip_sum(c):
        if c in S_ONLY:
            k = C * S_ONLY.index(c)
            act(lane(c), A("stmp", k, k + 16 * c), ACT.Relu, acc=A("rs", c, c + 1))
        elif c in V_SUM:
            reduce(A("rs", c, c + 1), lane(c), ALU.add)
        else:
            act(A("junk", 8 * c * (c - 1), 8 * c * (c + 1)), lane(c), ACT.Identity, acc=A("rs", c, c + 1))
    def quant_c(m): quant("c", TO[m], TO[m] + TW[m], A("ct", 4 * TO[m], 4 * (TO[m] + TW[m])))
    def sum_c(m): mm(2 + m // 3, "b", 0, "c", TO[m], TO[m] + TW[m], m in (0, 4), m in (2, 3))
    def shared(m): return [c for c in TILES[m] if c and c not in S_ONLY]
    def scores(h, w):
        quant("x", H * h, H * h + H, A("xt", 4 * H * h, 4 * H * h + 4 * H))
        mm(4 + 2 * h, w, 0, "x", H * h, H * h + H)
        if w == "u1": mm(5 + 2 * h, w, 0, "x", H * h, H * h + H)
    def spread(a): pick("uf", 128 * a, 128 * a + 128, "ul", 32 * a, 32 * a + 16, A("un", 0, 8), arr=[("arru", 4 * half)])
    def quant_e(b): quant("e", 128 * b, 128 * b + 128, A("et", 512 * b, 512 * b + 512))

    scores(0, "u1")
    mine = senders(rank)
    other = [[r for r in ((s + 1) % n, (s + 2) % n) if r != rank][0] for s in mine]
    place = [senders(d).index(s) for d, s in zip(other, mine)]
    pick("u2", 0, 16, "u0", 0, 128, A("u8", 0, 1))
    send([(d, T.q_u2[:, 0:16].bitcast(dt.uint8), T.q_ul[:, 32 * a:32 * a + 16].bitcast(dt.uint8), "arru") for d, a in zip(other, place)], [A("q_u2")])
    send([(d, T.s_u2[:, 0:16], T.s_ul[:, 32 * a:32 * a + 16], "arru") for d, a in zip(other, place)], [A("s_u2")])
    iota(A("q4"), [[0, 80], [1, 4]], 0, 0)
    iota(A("j192"), [[1, NS]], 1, 0)
    iota(A("ramp"), [[16, 16], [0, 16]], 0, 0)
    iota(A("r16"), [[0, TB // 16], [SM, 16]], 0, 0)
    for b in range(2): unit_tile(b)
    iota(A("rs4b"), [[0, 80], [2 * SM, 4]], -SM, 0)
    iota(A("ffp"), [[0, B1]], 0, 0)
    ts(A("ge"), A("jg"), pg, ALU.is_equal)
    memset(A("rs", 0, 1), 0.0)
    for b in range(4):
        act(A("bt", b, 512, 4), A("ge"), ACT.Copy)
    for t in range(R):
        lastr = t == R - 1
        act(A("ss", 0, H), PS(5, H), ACT.Copy)
        tt(A("xs", 0, H), PS(4, H), A("m16", 0, H), ALU.min)
        scores(1, "u1")
        act(A("ss", H, C), PS(7, H), ACT.Copy)
        hold(A("ys", 0, H), A("xs", 0, H), A("rs16", 0, H), -BIG)
        if t == 0:
            tt(A("pk", 1, 2), A("pj", 0, 1), A("pj", 3, 4), ALU.add)
            for k, most in enumerate((15.0, 3.0, 5.0)): ts(A("c3", k, k + 1), pr, most, ALU.min, 16.0, ALU.mult)
            ts(A("colr"), pr, -1.0, ALU.mult, 15.0 + 256, ALU.add)
        tt(A("xs", H, C), PS(6, H), A("m16", 0, H), ALU.min)
        first = [c for c in S_ONLY if 16 * c + 16 <= H]
        for c in first: strip(c)
        for c in first: strip_sum(c)
        tt(A("ct", 0, 4 * H, 4), A("ys", 0, H), PS(4, H), ALU.is_ge)
        hold(A("ys", H, C), A("xs", H, C), A("rs16", 0, H), -BIG)
        for c in shared(4): strip(c)
        rest = [c for c in S_ONLY if c not in first]
        for c in rest: strip(c)
        for c in rest: strip_sum(c)
        tt(A("ct", 4 * H, 4 * C, 4), A("ys", H, C), PS(6, H), ALU.is_ge)
        if t == 0: quant("b", 0, 128, A("bt"))
        done = [4]
        for m in range(4):
            for c in shared(m):
                strip(c)
                if c not in V_SUM: strip_sum(c)
                if done:
                    quant_c(done[0])
                    sum_c(done.pop(0))
            done.append(m)
        if t == 0:
            ts(A("m16h"), A("eq16"), 2.0 * SM, ALU.mult, -128.0 - SM, ALU.add)
        scan(A("rds"), A("rsd"), A("ct", 0, 4 * C, 4), SM, ALU.min, ALU.add)
        for m in done:
            quant_c(m)
            sum_c(m)
        tt(A("xc"), PS(2, C), A("m16h"), ALU.add)
        for c in V_SUM: strip_sum(c)
        if t == 0:
            for b in range(4): act(A("x32", C * b, C * b + C), A("xt", b, 4 * C, 4), ACT.Copy, scale=32.0)
            ts(A("pk", 2, 3), A("pk", 1, 2), 1, ALU.bitwise_and)
        tt(A("xd"), PS(3, 128), A("xc", 0, 128), ALU.add)
        hold(A("yc", 128), A("xc", 128), A("rs16b", 128))
        tt(A("w2"), A("rds", 15, C, 16), A("rs"), ALU.add)
        if t == 0:
            for k in range(R): memset(A("km%d" % k, 14, 15), -BIG)
        hold(A("yc", 0, 128), A("xd"), A("rs16b", 0, 128))
        if t == 0:
            ts(A("co"), A("pk", 2, 3), C + 16.0, ALU.mult, 15.0, ALU.add)
            ts(A("ca"), A("pk", 2, 3), L + 16.0, ALU.mult, 15.0, ALU.add)
        tt(A("rk"), A("yc", 15, C, 16), A("w2"), ALU.subtract)
        if t == 0:
            ts(A("lo", 0, 1), A("c3", 0, 1), A("co"), ALU.add)
            ts(A("la", 0, 1), A("c3", 2, 3), A("ca"), ALU.add)
            ts(A("lo", 1, 2), A("c3", 1, 2), A("co"), ALU.add, 256.0, ALU.add)
        ts(A("ofr"), A("rk"), A("colr"), ALU.add)
        if t == 0:
            quant_e(0)
            copy(A("un"), A("uo32"))
        scatter(A("ow", 16, 16 + C), A("ofr"), A("jb"))
        turn(A("ta", 0, L), A("ow", 16, 16 + L))
        turn(A("ta", L), A("ow", 0, L + 32))
        turn(A("tw", L, C), A("ow", 16 + L, 16 + C))
        ts(A("ofa"), IND(A("ta"), A("la", 0, 1)), 128.0, ALU.add)
        turn(A("tw", C + L), A("ow", L))
        def row_of(b, off): return IND(A("x32", C * b, C * b + C), off)
        for b in range(2):
            act(A("at", 2 + b, 4 * L, 4), row_of(2 + b, A("ofa", 0, L // 16)), ACT.Copy, scale=1.0 / 32)
            ts(A("at", b, 4 * L, 4), row_of(b, A("ofa", 0, L // 16)), 1.0 / 32, ALU.mult)
        ts(A("ofk"), IND(A("tw"), A("lo")), 128.0, ALU.add)
        stay = A("ofk", L // 16, C // 16)
        an, ln, km, kin = "a%d" % t, "l%d" % t, "km%d" % t, "kin%d" % t
        quant(an, 0, 128, A("at"))
        to = [(rank + 1) % n, (rank + 2) % n]
        at = [L * senders(d).index(rank) for d in to]
        send([(d, T["q_" + an][:, 0:L].bitcast(dt.uint8), T["q_" + ln][:, a:a + L].bitcast(dt.uint8), "arra%d" % t) for d, a in zip(to, at)], [A("q_" + an)])
        send([(d, T["s_" + an][:, 0:L], T["s_" + ln][:, a:a + L], "arra%d" % t) for d, a in zip(to, at)], [A("s_" + an)])
        copy(A("kf"), IND(A("ss"), stay))
        if t == 0:
            act(A("m16n"), A("eq16", 0, KEEP), ACT.Copy, scale=-2 * BIG)
        for b in range(4): act(A("vw", 4 * STAY + b, 4 * (STAY + KEEP), 4), row_of(b, stay), ACT.Copy, scale=1.0 / 64)
        if t == 0: spread(0)
        tt(A("sx", 0, 14), A("kf", 15, KEEP, 16), A("m16", 0, 14), ALU.min)
        scan(A("ky"), A("m16n"), A("kf"), -BIG, ALU.min, ALU.max)
        reduce(A(km, 15, 16), A("sx", 0, 14), ALU.max)
        copy(A(km, 0, 14), A("ky", 15, KEEP, 16))
        send([(d, T[km][:, 0:16], T[kin][:, 16 * a:16 * a + 16], "arrp%d" % t) for d, a in zip(other, place)], [A(km)])
        memset(A("ww"), 1.0)
        if t == 0:
            for b in range(2, 4): unit_tile(b)
            iota(A("rmw", MW * NSS), [[0, 12 - NSS], [SM, MW]], -2 * KEEP, 0)
            spread(1)
            memset(A("ms", NS + 1, 12 * MW, MW), 0.0)
            quant_e(1)
            ts(A("cl"), A("pk", 2, 3), NS + 16.0, ALU.mult, 15.0, ALU.add)
            ts(A("c2"), pr, 11.0, ALU.min, 16.0, ALU.mult)
            ts(A("lp", 0, 1), A("c2"), A("cl"), ALU.add)
        if t == 1:
            quant("v", 0, 128, A("vt"))
            memset(A("pl", 0, 1), 0.0)
            memset(A("pl", NS + 1, STAY), 0.0)
        copy(A("gt", 0, 4), A("vw", 4 * STAY, 4 * STAY + 4))
        def unpack(b):
            mm(4 + b, "e", 128 * b, ln, 0, NS)
            act(A("vw", 4 + b, 4 + 4 * NS, 4), PS(4 + b, NS), ACT.Copy, scale=0.5)
        mm(0, "u1", 0, ln, 0, NS, arr=[("arra%d" % t, 4 * half)])
        mm(1, "uf", 0, ln, 0, 128)
        mm(2, "uf", 128, ln, NS - 128, NS)
        views = [[(PS(0, NS), 0, NS, km, 0)], [(PS(1, L), 0, L, kin, 0), (PS(2, 128, 128 - L), L, NS, kin, 16)]]
        def runs(e):
            for s, lo, hi, w, a in views[e]:
                ts(A("b1", B1 * e + 16 + lo, B1 * e + 16 + hi), s, A(w, a + 15, a + 16), ALU.is_lt, arr=[("arrp%d" % t, 2 * half)] if e and not lo else ())
                act(A("sa", NS * e + lo, NS * e + hi), s, ACT.Copy)
        def turns(e):
            turn(A("t1", TB * e, TB * e + NS), A("b1", B1 * e + 16, B1 * e + 16 + NS))
            turn(A("t1", TB * e + NS, TB * e + TB), A("b1", B1 * e, B1 * e + B1))
        def sums(e):
            for lo, hi in ((0, NS), (NS, TB)):
                scan(A("s1", TB * e + lo, TB * e + hi), A("r16", lo, hi), A("t1", TB * e + lo, TB * e + hi), 0.0, ALU.min, ALU.add)
        def lists(e):
            ts(A("s16", 12 * e, 12 * e + 12), A("s1", TB * e + 15, TB * e + NS, 16), 16.0, ALU.mult)
            copy(A("ofb", 16 * e, 16 * e + 16), IND(A("s1", TB * e, TB * e + TB), A("lp", 0, 1)))
        def places(e):
            for s, lo, hi, w, a in views[e]:
                tt(A("b2", NS * e + lo, NS * e + hi), IND(A(w, a, a + 16), A("ofb", 16 * e + lo // 16, 16 * e + hi // 16)),
                   A("sa", NS * e + lo, NS * e + hi), ALU.is_gt)
        def turn2(e, lo, hi): turn(A("t2", NS * e + lo, NS * e + hi), A("b2", NS * e + lo, NS * e + hi))
        def sum2(e, lo, hi): scan(A("s2", NS * e + lo, NS * e + hi), A("r16", lo, hi), A("t2", NS * e + lo, NS * e + hi), 0.0, ALU.min, ALU.add)
        def total(e): tt(A("tot", 16 * e, 16 * e + 12), A("s2", NS * e + 15, NS * e + NS, 16), A("s16", 12 * e, 12 * e + 12), ALU.add)
        steps = [runs, turns, sums, lists, places]
        runs(0)
        for k in range(1, 5):
            steps[k](0)
            steps[k - 1](1)
            if k == 1:
                for b in range(4 if t else 2): unpack(b)
        if t == 0:
            act(A("q4"), A("q4"), ACT.Abs, scale=-1.0, bias=pe)
            act(A("k4"), A("q4"), ACT.Relu, scale=-1 / TINY, bias=1 / TINY)
            act(A("sid"), A("j192"), ACT.Copy, scale=TINY)
            for b in range(2, 4):
                quant_e(b)
                unpack(b)
        if t == 1:
            act(A("k16"), A("eq16"), ACT.Relu, scale=2 / TINY)
            act(A("pl", 1, NS + 1), A("j192"), ACT.Identity, bias=C - 1.0)
        if lastr:
            act(A("pl", STAY, STAY + KEEP), A("ow", 16 + L, 16 + C), ACT.Identity, bias=128.0)
        turn2(0, 0, NS)
        places(1)
        sum2(0, 0, NS)
        for lo in (0, L): turn2(1, lo, lo + L)
        total(0)
        for lo in (0, L): sum2(1, lo, lo + L)
        def spread_tot(e, lo): return IND(A("tot", 16 * e, 16 * e + 12), A("un", lo // 16, (lo + L) // 16))
        copy(A("fo", 0, L), spread_tot(0, 0))
        total(1)
        copy(A("fo", L, NS), spread_tot(0, L))
        if t == 0:
            ts(A("lev1", 0, NS), A("q16", 0, NS), pr, ALU.is_gt, 1.0 / 16, ALU.mult)
        for lo in (0, L): tt(A("fw", lo, lo + L), spread_tot(1, lo), A("fo", lo, lo + L), ALU.max)
        if t == 0: ts(A("lev1", NS), A("ramp", 0, NS), 1.0 / 256, ALU.mult, -KEEP / 2, ALU.add)
        ff = A("ffp", 16, 16 + NS)
        def keys(lo): tt(A("kk", lo, lo + L), A("ffp", 16 + lo, 16 + lo + L), A("lev", lo, lo + L), ALU.add)
        turn(A("ffp", 16, 16 + L), A("fw", 0, L))
        if t == 0: ts(A("iod"), A("ramp", 0, 256, 16), 1.0 / 256, ALU.mult, 1.0 / 32 - KEEP / 2, ALU.add)
        turn(A("ffp", 16 + L, 16 + NS), A("fw", L, NS))
        if t == 0: tt(A("lev"), A("lev1", 0, NS), A("lev1", NS), ALU.add)
        else: keys(0)
        turn(A("fw", NS, TB), A("ffp"))
        if t == 0: keys(0)
        keys(L)
        fd = IND(A("fw"), A("lp", 0, 1))
        tt(A("kd"), fd, A("iod"), ALU.add)
        def key(c): return A("kd", c, c + 1)
        for c in range(NSS):
            act(A("junk2", NS * c, NS * c + NS), A("kk"), ACT.Sign, scale=-1.0, bias=key(c), acc=A("acc", c, c + 1))
        if lastr:
            act(A("f32"), ff, ACT.Copy)
            dma("Y", T.ls[:, C:C + NS], rows("f32"), [A("f32")], [])
        ts(A("ms", NS, 16 * MW, MW), fd, float(KEEP - 1), ALU.min, 2.0, ALU.mult)
        for c in range(NSS, 12):
            ts(A("ms", MW * c, MW * c + NS), A("kk"), key(c), ALU.is_lt, 2.0, ALU.mult)
        for lo, hi in ((NSS, 10), (10, 12)):
            scan(A("mss", MW * lo, MW * hi), A("rmw", MW * lo, MW * hi), A("ms", MW * lo, MW * hi), 0.0, ALU.min, ALU.add)
        e = NSS - 1
        ts(A("hl"), A("ms", MW * e + NS, MW * e + NS + 1), 0.5, ALU.mult, NS / 2, ALU.add)
        tt(A("p2", 0, e), A("acc", 0, e), A("ms", NS, MW * e, MW), ALU.add)
        ts(A("ofp", NSS, 12), A("mss", MW * NSS + MW - 1, 12 * MW, MW), 0.5, ALU.mult, 1.0 * KEEP, ALU.add)
        ts(A("ofp", 0, e), A("p2", 0, e), 0.5, ALU.mult, NS / 2, ALU.add)
        ts(A("ofp", e, NSS), A("acc", e, NSS), 0.5, ALU.mult, A("hl"), ALU.add)
        scatter(A("ww"), A("ofp"), A("sid"))
        scan(A("cum"), A("one5", 0, C), A("ww", 0, C), STAY - 1, ALU.mult, ALU.add)
        halves = ((0, H), (H, C))
        for lo, hi in halves: tt(A("wm", lo, hi), A("ww", lo, hi), A("k4", lo, hi), ALU.mult)
        for lo, hi in halves: scan(A("wx", lo, hi), A("cum", lo, hi), A("wm", lo, hi), -SM, ALU.max, ALU.min)
        if t == 0: memset(A("vw", 0, 4), 0.0)
        for lo, hi in halves: hold(A("wy", lo, hi), A("wx", lo, hi), A("rs4b", lo, hi))
        if t == 0: memset(A("vw", 4 + 4 * NS, 4 * STAY), 0.0)
        for lo, hi in halves: ts(A("ofg", lo // 4, hi // 4), A("wy", lo + 3, hi, 4), 4.0, ALU.mult, p4, ALU.add)
        if lastr: tt(A("lx", 0, H), A("ww", 0, H), A("k16", 0, H), ALU.mult)
        def gathered(lo, hi): return A("gt", 16 * lo + 4, 16 * hi + 4), IND(A("vw"), A("ofg", lo, hi))
        def add(lo, hi): tt(A("zt", 16 * lo, 16 * hi), A("gt", 16 * lo + 4, 16 * hi + 4), A("gt", 16 * lo, 16 * hi), ALU.add)
        banks = [[4, 5, 6, 7], [0, 1, 2, 3]]
        def layer(h):
            quant("z", H * h, H * h + H, A("zt", 4 * H * h, 4 * H * h + 4 * H))
            for b in range(4): mm(banks[h][b], "w", 128 * b, "z", H * h, H * h + H)
        def part(name, h, b): return A(name, 4 * H * h + b, 4 * H * h + 4 * H, 4)
        def row(h, b): return A("x32", C * b + H * h, C * b + H * h + H)
        def summed(h, b): tt(row(h, b), PS(banks[h][b], H), part("z32", h, b), ALU.add)
        for lo, hi in GS: act(*gathered(lo, hi), ACT.Copy)
        for lo, hi in GV: copy(*gathered(lo, hi))
        for lo, hi in (GV + GS)[:-1]: add(lo, hi)
        layer(0)
        add(*GS[-1])
        if lastr: tt(A("lx", H, C), A("ww", H, C), A("k16", H, C), ALU.mult)
        for h in range(2):
            act(A("z32", 4 * H * h, 4 * H * h + 4 * H), A("zt", 4 * H * h, 4 * H * h + 4 * H), ACT.Copy, scale=32.0)
        summed(0, 0)
        layer(1)
        for h in range(2):
            for b in range(4):
                if h == 1 and b == 3: scores(0, "v" if lastr else "u1")
                if h or b: summed(h, b)
                if h == 0 or b < SD: act(part("xt", h, b), row(h, b), ACT.Copy, scale=1.0 / 32)
        for b in range(SD, 3): ts(part("xt", 1, b), row(1, b), 1.0 / 32, ALU.mult)
        if lastr: scan(A("lf"), A("cum"), A("lx"), -SM, ALU.max, ALU.min)
        ts(part("xt", 1, 3), row(1, 3), 1.0 / 32, ALU.mult)

    dma("Y", T.oc[:, 0:4 * H], T.q_x[:, 0:H].bitcast(dt.uint8), [A("q_x", 0, H)], [])
    act(A("yy", 0, H), PS(4, H), ACT.Copy)
    dma("S", T.y[:, 0:H], T.yy[:, 0:H], [A("yy", 0, H)], [])
    hold(A("ly"), A("lf"), A("rs16b"))
    scores(1, "v")
    dma("Y", T.oc[:, 4 * H:4 * C], T.q_x[:, H:C].bitcast(dt.uint8), [A("q_x", H, C)], [])
    copy(A("ofl"), A("ly", 15, C, 16))
    act(A("lso"), IND(A("pl"), A("ofl")), ACT.Copy)
    copy(A("yy", H, C), PS(6, H))
    for k in range(4):
        dma("Y", T.osc[4 * k:4 * k + 4, :], T.s_x[32 * k:32 * k + 4, :], [A("s_x")], [])
    dma("Y", T.y[:, H:C], T.yy[:, H:C], [A("yy", H, C)], [])
    dma("S", T.ls[:, 0:C], rows("lso"), [A("lso")], [])
    _emit(g, T, ops)
